import numpy as np
import ml_dtypes


def mxq(x, axis, fmt="e4m3"):
    dtype, down = {"e4m3": (ml_dtypes.float8_e4m3fn, 7), "e5m2": (ml_dtypes.float8_e5m2, 14)}[fmt]
    v = np.moveaxis(np.asarray(x, np.float32).astype(ml_dtypes.bfloat16).astype(np.float64), axis, -1)
    blocks = v.reshape(v.shape[:-1] + (-1, 32))
    amax = np.abs(blocks).max(-1, keepdims=True)
    byte = np.maximum(np.where(amax > 0, np.frexp(amax)[1] - 1 + 127, 0) - down, 1)
    scale = np.exp2(byte - 127.0)
    codes = (blocks / scale).astype(np.float32).astype(dtype).astype(np.float64)
    return np.moveaxis((codes * scale).reshape(v.shape), -1, axis)


WIDE = False


def mx_kscale(k):
    if not WIDE:
        return np.ones(k)
    levels = np.array([24, -24, 12, -12, 0])
    if k % 512:
        return np.exp2(np.random.permutation(np.resize(levels, k // 32))).repeat(32)
    a = np.empty((k // 512, 16))
    for p in range(k // 512):
        a[p, :8] = np.random.permutation(np.resize(levels, 8))
        for g in range(8):
            far = levels[np.abs(levels - a[p, g]) >= 10]
            a[p, g + 8] = far[np.random.randint(len(far))]
    return np.exp2(a.ravel()).repeat(32)


def f64(x):
    return np.asarray(x).astype(np.float64)


def striped(idx):
    return np.tile(idx.reshape(-1, 16).T, (8, 1)).astype(np.uint16)


def unstriped(offs):
    return offs[:16].T.reshape(-1).astype(np.int64)


E2M1 = np.array([0.0, 0.5, 1.0, 1.5, 2.0, 3.0, 4.0, 6.0, -0.0, -0.5, -1.0, -1.5, -2.0, -3.0, -4.0, -6.0])


def pack_weight(w, fmt):
    k, n = w.shape
    w = f64(np.asarray(w, np.float32).astype(ml_dtypes.bfloat16)).reshape(k // 32, 32, n)
    amax = np.abs(w).max(1)
    if fmt == "e4m3":
        byte = np.frexp(amax)[1] - 1 + 127 - 7
    else:
        mant, ex = np.frexp(amax / 6.0)
        byte = np.where(mant > 0.5, ex, ex - 1) + 127
    byte = np.clip(np.where(amax > 0, byte, 1), 1, 254)
    scaled = (w * np.exp2(127.0 - byte)[:, None, :]).reshape(k, n).astype(np.float32)
    by_word = np.ascontiguousarray(scaled.reshape(k // 512, 128, 4, n).transpose(0, 1, 3, 2))
    if fmt == "e4m3":
        words = by_word.astype(ml_dtypes.float8_e4m3fn).view(np.uint8)
    else:
        c = by_word.astype(ml_dtypes.float4_e2m1fn).view(np.uint8) & 0xF
        words = (c[..., 0::2] | (c[..., 1::2] << 4)).reshape(k // 512, 128, 2 * n)
    return np.ascontiguousarray(words), np.ascontiguousarray(byte.astype(np.uint8).reshape(k // 512, 16, n))


def unpack_weight(words, scales, fmt):
    g, _, n = scales.shape
    words = np.ascontiguousarray(words).reshape(g, 128, n, -1)
    if fmt == "e4m3":
        vals = words.view(ml_dtypes.float8_e4m3fn).astype(np.float64)
    else:
        nib = np.empty((g, 128, n, 4), np.uint8)
        nib[..., 0::2] = words & 0xF
        nib[..., 1::2] = words >> 4
        vals = E2M1[nib]
    vals = vals * np.repeat(np.exp2(scales.astype(np.float64) - 127.0), 8, axis=1)[..., None]
    return vals.transpose(0, 1, 3, 2).reshape(g * 512, n)


def pack_table4(v):
    words, scales = pack_weight(v, "e2m1")
    g, t = words.shape[0] // 2, v.shape[1]
    return np.ascontiguousarray(words.reshape(g, 2, 128, t, 2).transpose(0, 2, 3, 1, 4).reshape(g, 128, t, 4)), scales


def unpack_table4(words, scales):
    g, _, t, _ = words.shape
    return unpack_weight(words.reshape(g, 128, t, 2, 2).transpose(0, 3, 1, 2, 4).reshape(2 * g, 128, 2 * t), scales, "e2m1")


K, R, N, T, J = 1024, 512, 512, 2048, 1024


def setup_inputs():
    n = np.random.standard_normal
    s = mx_kscale(K)[:, None]
    u = mx_kscale(R)[:, None]
    wd = n((R, N)) / np.sqrt(R) / u
    wd4 = pack_weight(wd, "e2m1")
    wdrest = wd - unpack_weight(*wd4, "e2m1")
    p_tab = pack_table4(n((K, T)) * s)
    p_ws = pack_weight(n((K, R)) / np.sqrt(2 * K) / s, "e2m1")
    p_wt = pack_weight(n((K, R)) / np.sqrt(2 * K) / s, "e2m1")
    p_wd8 = pack_weight(wdrest, "e4m3")
    return {
        "tab_words": p_tab[0],
        "tab_scales": p_tab[1],
        "ws_words": p_ws[0],
        "ws_scales": p_ws[1],
        "wt_words": p_wt[0],
        "wt_scales": p_wt[1],
        "sm": (np.random.uniform(0.5, 2.0, R) * u[:, 0]).astype(np.float32),
        "wd4_words": wd4[0],
        "wd4_scales": wd4[1],
        "wd8_words": p_wd8[0],
        "wd8_scales": p_wd8[1],
        "gT": (n((N, T))).astype(np.float32),
        "wgo": np.tile(np.random.uniform(0.5, 2.0, J), (128, 1)).astype(np.float32),
        "offs": striped(np.random.permutation(T)[:J]),
        "offs2": striped(np.random.permutation(T)[:J]),
    }


def reference(tab_words, tab_scales, ws_words, ws_scales, wt_words, wt_scales, sm, wd4_words, wd4_scales, wd8_words, wd8_scales, gT, wgo, offs, offs2):
    idx = unstriped(offs)
    idx2 = unstriped(offs2)
    tab_ = unpack_table4(tab_words, tab_scales)[:, idx]
    tabb_ = unpack_table4(tab_words, tab_scales)[:, idx2]
    ws_ = unpack_weight(ws_words, ws_scales, "e2m1")
    wt_ = unpack_weight(wt_words, wt_scales, "e2m1")
    a = ws_.T @ tab_ + wt_.T @ tabb_
    h = f64(sm)[:, None] * np.tanh(a)
    h_ = mxq(h, 0, "e4m3")
    wd4_ = unpack_weight(wd4_words, wd4_scales, "e2m1")
    wd8_ = unpack_weight(wd8_words, wd8_scales, "e4m3")
    y = wd4_.T @ h_ + wd8_.T @ h_
    out = np.zeros((N, T))
    out[:, idx2] = f64(wgo)[0] * (y * f64(gT)[:, idx])
    return out

@@ -1,0 +1,207 @@
+from contextlib import ExitStack
+
+import concourse.mybir as mybir
+
+K, R, N, T, J = 1024, 512, 512, 2048, 1024
+FLOPS = 2 * J * (2 * K * R + 2 * R * N)
+
+F32 = mybir.dt.float32
+BF16 = mybir.dt.bfloat16
+I32 = mybir.dt.int32
+U32 = mybir.dt.uint32
+U16 = mybir.dt.uint16
+U8 = mybir.dt.uint8
+FP8X4 = mybir.dt.float8_e4m3fn_x4
+FP4X4 = mybir.dt.float4_e2m1fn_x4
+MULT = mybir.AluOpType.mult
+TANH = mybir.ActivationFunctionType.Tanh
+COPY = mybir.ActivationFunctionType.Copy
+
+P = 128
+PACK = 4
+PASSES = K // (P * PACK)
+QUADS = 4
+CH = 512
+CHUNKS = J // CH
+LIST_COLS = J // 16
+CH_COLS = CH // 16
+N_TILES = N // P
+WINDOWS = 3
+
+
+def tile_list_msg_tanh_res_gate_kernel(
+    tc, tab_words, tab_scales, ws_words, ws_scales, wt_words, wt_scales, sm,
+    wd4_words, wd4_scales, wd8_words, wd8_scales, gT, wgo, offs, offs2, out,
+):
+    nc = tc.nc
+    with ExitStack() as ctx:
+        keep = ctx.enter_context(tc.tile_pool(name="keep", bufs=1))
+        ring = ctx.enter_context(tc.tile_pool(name="ring", bufs=2))
+        psum_a = ctx.enter_context(tc.psum_pool(name="psum_a", bufs=4))
+        psum_y = ctx.enter_context(tc.psum_pool(name="psum_y", bufs=4))
+
+        src_list = keep.tile([P, LIST_COLS], U16, name="src_list")
+        dst_list = keep.tile([P, LIST_COLS], U16, name="dst_list")
+        nc.sync.dma_start(src_list[:], offs)
+        nc.sync.dma_start(dst_list[:], offs2)
+        lists = (src_list, dst_list)
+
+        tab_sc = keep.tile([P, T // 4], I32, name="tab_sc", align_bytes=64)
+        nc.vector.memset(tab_sc[:], 0)
+        for q in range(QUADS):
+            nc.sync.dma_start(
+                tab_sc[32 * q : 32 * q + 4 * PASSES, :],
+                tab_scales[:, 4 * q : 4 * q + 4, :].bitcast(I32),
+            )
+
+        w1_sc_raw = keep.tile([P, 2, PASSES, R // 4], I32, name="w1_sc_raw", align_bytes=64)
+        nc.vector.memset(w1_sc_raw[:], 0)
+        w1_raw = keep.tile([P, 2, PASSES, R // 2], I32, name="w1_raw", align_bytes=64)
+        for w, words in enumerate((ws_words, wt_words)):
+            nc.sync.dma_start(w1_raw[:, w, :, :], words.rearrange("a p n -> p a n").bitcast(I32))
+        for w, scales in enumerate((ws_scales, wt_scales)):
+            for q in range(QUADS):
+                nc.sync.dma_start(
+                    w1_sc_raw[32 * q : 32 * q + 4, w, :, :],
+                    scales[:, 4 * q : 4 * q + 4, :].rearrange("a q n -> q a n").bitcast(I32),
+                )
+
+        table = keep.tile([P, T], I32, name="table", align_bytes=64)
+        nc.sync.dma_start(table[:], tab_words[0].rearrange("p t b -> p (t b)").bitcast(I32))
+
+        sm_sb = keep.tile([P, PACK], F32, name="sm_sb")
+        nc.sync.dma_start(sm_sb[:], sm.rearrange("(p t) -> p t", t=PACK))
+        wgo_sb = keep.tile([P, J], F32, name="wgo_sb")
+        nc.sync.dma_start(wgo_sb[:], wgo)
+        g_sb = []
+        for nt in range(N_TILES):
+            g_tile = keep.tile([P, T], F32, name=f"g{nt}")
+            nc.sync.dma_start(g_tile[:], gT[nt * P : (nt + 1) * P, :])
+            g_sb.append(g_tile)
+
+        wd_sc = keep.tile([P, 2, N // 4], I32, name="wd_sc", align_bytes=64)
+        nc.gpsimd.memset(wd_sc[:], 0)
+        for w, scales in enumerate((wd4_scales, wd8_scales)):
+            for q in range(QUADS):
+                nc.gpsimd.dma_start(
+                    wd_sc[32 * q : 32 * q + 4, w, :], scales[0, 4 * q : 4 * q + 4, :].bitcast(I32)
+                )
+        wd4 = keep.tile([P, N // 2], I32, name="wd4", align_bytes=64)
+        wd8 = keep.tile([P, N], I32, name="wd8", align_bytes=64)
+        nc.sync.dma_start(wd4[:], wd4_words[0].bitcast(I32))
+        nc.sync.dma_start(wd8[:], wd8_words[0].rearrange("p n i -> p (n i)").bitcast(I32))
+
+        v_sc = []
+        for s, lst in enumerate(lists):
+            moved = keep.tile([P, J // 4], I32, name=f"v_sc_moved{s}", align_bytes=64)
+            nc.vector.memset(moved[:], 0)
+            picked = keep.tile([P, J // 4], I32, name=f"v_sc_picked{s}", align_bytes=64)
+            nc.vector.tensor_copy(picked[:].bitcast(U8), tab_sc[:].bitcast(U8).indirect(lst[:]))
+            nc.scalar.dma_start(moved[0 : P - 4, :], picked[4:P, :])
+            v_sc.append((picked, moved))
+
+        windows = [keep.tile([P, T], F32, name=f"window{i}") for i in range(WINDOWS)]
+        nc.vector.memset(windows[0][:], 0.0)
+        nc.vector.memset(windows[1][:], 0.0)
+
+        w1 = keep.tile([P, 2 * PASSES, PACK, P], U16, name="w1", align_bytes=64)
+        w1_sc = keep.tile([P, 2 * PASSES, PACK, P], U8, name="w1_sc", align_bytes=64)
+        nc.vector.tensor_copy(
+            w1[:],
+            w1_raw[:].rearrange("p w a n -> p (w a n)").bitcast(U16).rearrange("p (c m t) -> p c t m", t=PACK, m=P),
+        )
+        nc.vector.tensor_copy(
+            w1_sc[:],
+            w1_sc_raw[:].rearrange("p w a n -> p (w a n)").bitcast(U8).rearrange("p (c m t) -> p c t m", t=PACK, m=P),
+        )
+
+        h_codes = keep.tile([P, J], U32, name="h_codes", align_bytes=64)
+        h_sc = keep.tile([P, J], U8, name="h_sc", align_bytes=64)
+
+        grouped = []
+        for c in range(CHUNKS):
+            cols = slice(c * CH, (c + 1) * CH)
+            v_words = []
+            for s, lst in enumerate(lists):
+                both = ring.tile([P, CH], U32, name=f"both{s}", align_bytes=64)
+                nc.vector.tensor_copy(
+                    both[:], table[:].bitcast(U32).indirect(lst[:, c * CH_COLS : (c + 1) * CH_COLS])
+                )
+                v_words.append(both)
+            parted = []
+            for s in range(2):
+                apart = ring.tile([P, PASSES, CH], U16, name=f"apart{s}", align_bytes=64)
+                nc.vector.tensor_copy(apart[:], v_words[s][:].bitcast(U16).rearrange("p (j d) -> p d j", d=PASSES))
+                parted.append(apart)
+
+            h_rows = ring.tile([P, PACK, CH], BF16, name="h_rows", align_bytes=64)
+            for t in range(PACK):
+                acc = psum_a.tile([P, CH], F32, name="acc")
+                for s in range(2):
+                    for a in range(PASSES):
+                        nc.tensor.matmul_mx(
+                            out=acc[:],
+                            lhsT=w1[:, PASSES * s + a, t, :].bitcast(FP4X4),
+                            lhsT_scale=w1_sc[:, PASSES * s + a, t, :],
+                            rhs=parted[s][:, a, :].bitcast(FP4X4),
+                            rhs_scale=v_sc[s][a][:].bitcast(U8)[:, cols],
+                            start=(s == 0 and a == 0),
+                            stop=(s == 1 and a == PASSES - 1),
+                        )
+                th = ring.tile([P, CH], F32, name="th")
+                nc.scalar.activation(th[:], acc[:], TANH)
+                nc.scalar.activation(h_rows[:, t, :], th[:], COPY, scale=sm_sb[:, t : t + 1])
+            h_grouped = ring.tile([P, CH, PACK], BF16, name="h_grouped", align_bytes=64)
+            nc.scalar.copy(h_grouped[:], h_rows[:].rearrange("p t j -> p j t"))
+            grouped.append(h_grouped)
+
+        gates = []
+        for nt in range(N_TILES):
+            gate = keep.tile([P, J], F32, name=f"gate{nt}")
+            gates.append(gate)
+
+        for c in range(CHUNKS):
+            cols = slice(c * CH, (c + 1) * CH)
+            nc.vector.quantize_mx(
+                out=h_codes[:, cols].bitcast(FP8X4),
+                scales=h_sc[:, cols],
+                in_=grouped[c][:].rearrange("p j t -> p (j t)"),
+            )
+
+        for nt in range(N_TILES):
+            nc.vector.tensor_tensor(gates[nt][:], g_sb[nt][:].indirect(src_list[:]), wgo_sb[:], MULT)
+
+        nc.vector.memset(windows[2][:], 0.0)
+        for nt in range(N_TILES):
+            rows = slice(nt * P, (nt + 1) * P)
+            window = windows[nt % WINDOWS]
+            msgs = []
+            for c in range(CHUNKS):
+                cols = slice(c * CH, (c + 1) * CH)
+                y = psum_y.tile([P, CH], F32, name="y")
+                nc.tensor.matmul_mx(
+                    out=y[:],
+                    lhsT=wd4[:, nt * P // 2 : (nt + 1) * P // 2].bitcast(FP4X4),
+                    lhsT_scale=wd_sc[:, 0, :].bitcast(U8)[:, rows],
+                    rhs=h_codes[:, cols].bitcast(FP8X4),
+                    rhs_scale=h_sc[:, cols],
+                    start=True,
+                    stop=False,
+                )
+                nc.tensor.matmul_mx(
+                    out=y[:],
+                    lhsT=wd8[:, rows].bitcast(FP8X4),
+                    lhsT_scale=wd_sc[:, 1, :].bitcast(U8)[:, rows],
+                    rhs=h_codes[:, cols].bitcast(FP8X4),
+                    rhs_scale=h_sc[:, cols],
+                    start=False,
+                    stop=True,
+                )
+                msg = ring.tile([P, CH], F32, name=f"msg{c}")
+                nc.vector.tensor_tensor(msg[:], y[:], gates[nt][:, cols], MULT)
+                msgs.append(msg)
+            for c in range(CHUNKS):
+                nc.vector.tensor_copy(
+                    window[:].indirect(dst_list[:, c * CH_COLS : (c + 1) * CH_COLS]), msgs[c][:]
+                )
+            nc.sync.dma_start(out[rows, :], window[:])

@@ -37,7 +37,8 @@ def tile_list_msg_tanh_res_gate_kernel(
     with ExitStack() as ctx:
         keep = ctx.enter_context(tc.tile_pool(name="keep", bufs=1))
         ring = ctx.enter_context(tc.tile_pool(name="ring", bufs=2))
-        psum_a = ctx.enter_context(tc.psum_pool(name="psum_a", bufs=4))
+        msgs = ctx.enter_context(tc.tile_pool(name="msgs", bufs=4))
+        psum_a = ctx.enter_context(tc.psum_pool(name="psum_a", bufs=1))
         psum_y = ctx.enter_context(tc.psum_pool(name="psum_y", bufs=4))
 
         src_list = keep.tile([P, LIST_COLS], U16, name="src_list")
@@ -48,24 +49,23 @@ def tile_list_msg_tanh_res_gate_kernel(
 
         tab_sc = keep.tile([P, T // 4], I32, name="tab_sc", align_bytes=64)
         nc.vector.memset(tab_sc[:], 0)
-        for q in range(QUADS):
+        for r in range(4):
             nc.sync.dma_start(
-                tab_sc[32 * q : 32 * q + 4 * PASSES, :],
-                tab_scales[:, 4 * q : 4 * q + 4, :].bitcast(I32),
+                tab_sc[r:P:16, :], tab_scales.rearrange("a (q r) t -> r q a t", r=4)[r].bitcast(I32)
             )
-
-        w1_sc_raw = keep.tile([P, 2, PASSES, R // 4], I32, name="w1_sc_raw", align_bytes=64)
+        w1_sc_raw = keep.tile([P, R // 4], I32, name="w1_sc_raw", tag="wd_sc", align_bytes=64)
         nc.vector.memset(w1_sc_raw[:], 0)
-        w1_raw = keep.tile([P, 2, PASSES, R // 2], I32, name="w1_raw", align_bytes=64)
-        for w, words in enumerate((ws_words, wt_words)):
-            nc.sync.dma_start(w1_raw[:, w, :, :], words.rearrange("a p n -> p a n").bitcast(I32))
         for w, scales in enumerate((ws_scales, wt_scales)):
-            for q in range(QUADS):
+            for r in range(4):
                 nc.sync.dma_start(
-                    w1_sc_raw[32 * q : 32 * q + 4, w, :, :],
-                    scales[:, 4 * q : 4 * q + 4, :].rearrange("a q n -> q a n").bitcast(I32),
+                    w1_sc_raw[8 * w + r : P : 16, :],
+                    scales.rearrange("a (q r) n -> r q a n", r=4)[r].bitcast(I32),
                 )
-
+        w1_raw = []
+        for w, words in enumerate((ws_words, wt_words)):
+            raw = keep.tile([P, PASSES, R // 2], I32, name=f"w1_raw{w}", tag=f"g{w}", align_bytes=64)
+            nc.sync.dma_start(raw[:], words.rearrange("a p n -> p a n").bitcast(I32))
+            w1_raw.append(raw)
         table = keep.tile([P, T], I32, name="table", align_bytes=64)
         nc.sync.dma_start(table[:], tab_words[0].rearrange("p t b -> p (t b)").bitcast(I32))
 
@@ -73,135 +73,169 @@ def tile_list_msg_tanh_res_gate_kernel(
         nc.sync.dma_start(sm_sb[:], sm.rearrange("(p t) -> p t", t=PACK))
         wgo_sb = keep.tile([P, J], F32, name="wgo_sb")
         nc.sync.dma_start(wgo_sb[:], wgo)
-        g_sb = []
-        for nt in range(N_TILES):
-            g_tile = keep.tile([P, T], F32, name=f"g{nt}")
-            nc.sync.dma_start(g_tile[:], gT[nt * P : (nt + 1) * P, :])
-            g_sb.append(g_tile)
-
-        wd_sc = keep.tile([P, 2, N // 4], I32, name="wd_sc", align_bytes=64)
-        nc.gpsimd.memset(wd_sc[:], 0)
-        for w, scales in enumerate((wd4_scales, wd8_scales)):
-            for q in range(QUADS):
-                nc.gpsimd.dma_start(
-                    wd_sc[32 * q : 32 * q + 4, w, :], scales[0, 4 * q : 4 * q + 4, :].bitcast(I32)
-                )
         wd4 = keep.tile([P, N // 2], I32, name="wd4", align_bytes=64)
         wd8 = keep.tile([P, N], I32, name="wd8", align_bytes=64)
         nc.sync.dma_start(wd4[:], wd4_words[0].bitcast(I32))
         nc.sync.dma_start(wd8[:], wd8_words[0].rearrange("p n i -> p (n i)").bitcast(I32))
 
+        v_moved = keep.tile([P, 2, J // 4], I32, name="v_moved", align_bytes=64)
+        w_moved = keep.tile([P, 2 * PASSES - 1, R // 4], I32, name="w_moved", align_bytes=64)
+        nc.vector.memset(v_moved[:], 0)
+        nc.vector.memset(w_moved[:], 0)
+
+        def shift(moved, source, rows_up):
+            count = P - max(rows_up, 16)
+            nc.scalar.dma_start(moved[0:count, :], source[rows_up : rows_up + count, :])
+
         v_sc = []
         for s, lst in enumerate(lists):
-            moved = keep.tile([P, J // 4], I32, name=f"v_sc_moved{s}", align_bytes=64)
-            nc.vector.memset(moved[:], 0)
             picked = keep.tile([P, J // 4], I32, name=f"v_sc_picked{s}", align_bytes=64)
             nc.vector.tensor_copy(picked[:].bitcast(U8), tab_sc[:].bitcast(U8).indirect(lst[:]))
-            nc.scalar.dma_start(moved[0 : P - 4, :], picked[4:P, :])
-            v_sc.append((picked, moved))
+            shift(v_moved[:, s, :], picked, 16)
+            v_sc.append((picked[:], v_moved[:, s, :]))
 
-        windows = [keep.tile([P, T], F32, name=f"window{i}") for i in range(WINDOWS)]
-        nc.vector.memset(windows[0][:], 0.0)
-        nc.vector.memset(windows[1][:], 0.0)
-
+        w1_sc_packed = keep.tile([P, R // 4], I32, name="w1_sc_packed", align_bytes=64)
+        nc.vector.tensor_copy(
+            w1_sc_packed[:].bitcast(U8).rearrange("p (t m) -> p t m", t=PACK),
+            w1_sc_raw[:].bitcast(U8).rearrange("p (m t) -> p t m", t=PACK),
+        )
+        w1_sc = [w1_sc_packed[:]]
+        for i in range(1, 2 * PASSES):
+            shift(w_moved[:, i - 1, :], w1_sc_packed, 8 * (i // PASSES) + 16 * (i % PASSES))
+            w1_sc.append(w_moved[:, i - 1, :])
         w1 = keep.tile([P, 2 * PASSES, PACK, P], U16, name="w1", align_bytes=64)
-        w1_sc = keep.tile([P, 2 * PASSES, PACK, P], U8, name="w1_sc", align_bytes=64)
-        nc.vector.tensor_copy(
-            w1[:],
-            w1_raw[:].rearrange("p w a n -> p (w a n)").bitcast(U16).rearrange("p (c m t) -> p c t m", t=PACK, m=P),
-        )
-        nc.vector.tensor_copy(
-            w1_sc[:],
-            w1_sc_raw[:].rearrange("p w a n -> p (w a n)").bitcast(U8).rearrange("p (c m t) -> p c t m", t=PACK, m=P),
-        )
+        for w in range(2):
+            nc.vector.tensor_copy(
+                w1[:, PASSES * w : PASSES * (w + 1), :, :],
+                w1_raw[w][:].bitcast(U16).rearrange("p a (m t) -> p a t m", t=PACK),
+            )
 
-        h_codes = keep.tile([P, J], U32, name="h_codes", align_bytes=64)
-        h_sc = keep.tile([P, J], U8, name="h_sc", align_bytes=64)
+        wd_sc = keep.tile([P, 2, N // 4], I32, name="wd_sc", tag="wd_sc", align_bytes=64)
+        nc.vector.memset(wd_sc[:], 0)
+        for w, scales in enumerate((wd4_scales, wd8_scales)):
+            for q in range(QUADS):
+                nc.scalar.dma_start(
+                    wd_sc[32 * q : 32 * q + 4, w, :], scales[0, 4 * q : 4 * q + 4, :].bitcast(I32)
+                )
 
-        grouped = []
-        for c in range(CHUNKS):
-            cols = slice(c * CH, (c + 1) * CH)
-            v_words = []
+        gates = [keep.tile([P, J], F32, name=f"gate{nt}") for nt in range(N_TILES)]
+
+        def look_up(c):
+            picked_words = []
             for s, lst in enumerate(lists):
-                both = ring.tile([P, CH], U32, name=f"both{s}", align_bytes=64)
+                both = keep.tile([P, CH], U32, name=f"both{c}{s}", tag=f"g{2 + 2 * c + s}", align_bytes=64)
                 nc.vector.tensor_copy(
                     both[:], table[:].bitcast(U32).indirect(lst[:, c * CH_COLS : (c + 1) * CH_COLS])
                 )
-                v_words.append(both)
+                picked_words.append(both)
             parted = []
             for s in range(2):
                 apart = ring.tile([P, PASSES, CH], U16, name=f"apart{s}", align_bytes=64)
-                nc.vector.tensor_copy(apart[:], v_words[s][:].bitcast(U16).rearrange("p (j d) -> p d j", d=PASSES))
+                nc.vector.tensor_copy(
+                    apart[:], picked_words[s][:].bitcast(U16).rearrange("p (j d) -> p d j", d=PASSES)
+                )
                 parted.append(apart)
+            return parted
 
+        def hidden(c, parted):
+            cols = slice(c * CH, (c + 1) * CH)
             h_rows = ring.tile([P, PACK, CH], BF16, name="h_rows", align_bytes=64)
             for t in range(PACK):
-                acc = psum_a.tile([P, CH], F32, name="acc")
-                for s in range(2):
-                    for a in range(PASSES):
-                        nc.tensor.matmul_mx(
-                            out=acc[:],
-                            lhsT=w1[:, PASSES * s + a, t, :].bitcast(FP4X4),
-                            lhsT_scale=w1_sc[:, PASSES * s + a, t, :],
-                            rhs=parted[s][:, a, :].bitcast(FP4X4),
-                            rhs_scale=v_sc[s][a][:].bitcast(U8)[:, cols],
-                            start=(s == 0 and a == 0),
-                            stop=(s == 1 and a == PASSES - 1),
-                        )
+                acc = psum_a.tile([P, CH], F32, name="acc", tag=f"a{t}")
+                for i in range(2 * PASSES):
+                    s, a = divmod(i, PASSES)
+                    nc.tensor.matmul_mx(
+                        out=acc[:],
+                        lhsT=w1[:, i, t, :].bitcast(FP4X4),
+                        lhsT_scale=w1_sc[i].bitcast(U8)[:, t * P : (t + 1) * P],
+                        rhs=parted[s][:, a, :].bitcast(FP4X4),
+                        rhs_scale=v_sc[s][a].bitcast(U8)[:, cols],
+                        start=(i == 0),
+                        stop=(i == 2 * PASSES - 1),
+                    )
                 th = ring.tile([P, CH], F32, name="th")
                 nc.scalar.activation(th[:], acc[:], TANH)
                 nc.scalar.activation(h_rows[:, t, :], th[:], COPY, scale=sm_sb[:, t : t + 1])
             h_grouped = ring.tile([P, CH, PACK], BF16, name="h_grouped", align_bytes=64)
             nc.scalar.copy(h_grouped[:], h_rows[:].rearrange("p t j -> p j t"))
-            grouped.append(h_grouped)
+            return h_grouped
 
-        gates = []
-        for nt in range(N_TILES):
-            gate = keep.tile([P, J], F32, name=f"gate{nt}")
-            gates.append(gate)
-
-        for c in range(CHUNKS):
+        def quantise(c, h_grouped):
             cols = slice(c * CH, (c + 1) * CH)
             nc.vector.quantize_mx(
                 out=h_codes[:, cols].bitcast(FP8X4),
                 scales=h_sc[:, cols],
-                in_=grouped[c][:].rearrange("p j t -> p (j t)"),
+                in_=h_grouped[:].rearrange("p j t -> p (j t)"),
             )
 
-        for nt in range(N_TILES):
+        def gate(nt):
             nc.vector.tensor_tensor(gates[nt][:], g_sb[nt][:].indirect(src_list[:]), wgo_sb[:], MULT)
 
-        nc.vector.memset(windows[2][:], 0.0)
-        for nt in range(N_TILES):
+        def message(nt, c, y):
             rows = slice(nt * P, (nt + 1) * P)
-            window = windows[nt % WINDOWS]
-            msgs = []
-            for c in range(CHUNKS):
-                cols = slice(c * CH, (c + 1) * CH)
-                y = psum_y.tile([P, CH], F32, name="y")
-                nc.tensor.matmul_mx(
-                    out=y[:],
-                    lhsT=wd4[:, nt * P // 2 : (nt + 1) * P // 2].bitcast(FP4X4),
-                    lhsT_scale=wd_sc[:, 0, :].bitcast(U8)[:, rows],
-                    rhs=h_codes[:, cols].bitcast(FP8X4),
-                    rhs_scale=h_sc[:, cols],
-                    start=True,
-                    stop=False,
-                )
-                nc.tensor.matmul_mx(
-                    out=y[:],
-                    lhsT=wd8[:, rows].bitcast(FP8X4),
-                    lhsT_scale=wd_sc[:, 1, :].bitcast(U8)[:, rows],
-                    rhs=h_codes[:, cols].bitcast(FP8X4),
-                    rhs_scale=h_sc[:, cols],
-                    start=False,
-                    stop=True,
-                )
-                msg = ring.tile([P, CH], F32, name=f"msg{c}")
-                nc.vector.tensor_tensor(msg[:], y[:], gates[nt][:, cols], MULT)
-                msgs.append(msg)
-            for c in range(CHUNKS):
-                nc.vector.tensor_copy(
-                    window[:].indirect(dst_list[:, c * CH_COLS : (c + 1) * CH_COLS]), msgs[c][:]
-                )
-            nc.sync.dma_start(out[rows, :], window[:])
+            cols = slice(c * CH, (c + 1) * CH)
+            nc.tensor.matmul_mx(
+                out=y[:],
+                lhsT=wd4[:, nt * P // 2 : (nt + 1) * P // 2].bitcast(FP4X4),
+                lhsT_scale=wd_sc[:, 0, :].bitcast(U8)[:, rows],
+                rhs=h_codes[:, cols].bitcast(FP8X4),
+                rhs_scale=h_sc[:, cols],
+                start=True,
+                stop=False,
+            )
+            nc.tensor.matmul_mx(
+                out=y[:],
+                lhsT=wd8[:, rows].bitcast(FP8X4),
+                lhsT_scale=wd_sc[:, 1, :].bitcast(U8)[:, rows],
+                rhs=h_codes[:, cols].bitcast(FP8X4),
+                rhs_scale=h_sc[:, cols],
+                start=False,
+                stop=True,
+            )
+            y_sb = msgs.tile([P, CH], F32, name="y_sb")
+            nc.scalar.copy(y_sb[:], y[:])
+            return y_sb
+
+        def scatter(nt, c, y_sb):
+            nc.vector.tensor_tensor(
+                windows[nt % WINDOWS][:].indirect(dst_list[:, c * CH_COLS : (c + 1) * CH_COLS]),
+                y_sb[:],
+                gates[nt][:, c * CH : (c + 1) * CH],
+                MULT,
+            )
+            if c == CHUNKS - 1:
+                nc.sync.dma_start(out[nt * P : (nt + 1) * P, :], windows[nt % WINDOWS][:])
+
+        def bank():
+            return psum_y.tile([P, CH], F32, name="y")
+
+        parted_0 = look_up(0)
+        parted_1 = look_up(1)
+        g_sb = []
+        for nt in range(N_TILES):
+            g_tile = keep.tile([P, T], F32, name=f"g{nt}", tag=f"g{nt}", align_bytes=64)
+            nc.sync.dma_start(g_tile[:], gT[nt * P : (nt + 1) * P, :])
+            g_sb.append(g_tile)
+        windows = [keep.tile([P, T], F32, name="window0")]
+        nc.vector.memset(windows[0][:], 0.0)
+
+        h_0 = hidden(0, parted_0)
+        for nt in range(WINDOWS):
+            gate(nt)
+            if nt + 1 < WINDOWS:
+                window = keep.tile([P, T], F32, name=f"window{nt + 1}", tag=f"g{nt}", align_bytes=64)
+                nc.gpsimd.memset(window[:], 0.0)
+                windows.append(window)
+        h_codes = keep.tile([P, J], U32, name="h_codes", tag="g2", align_bytes=64)
+        h_sc = keep.tile([P, J], U8, name="h_sc", align_bytes=64)
+        quantise(0, h_0)
+        y_00 = message(0, 0, bank())
+        y_10 = message(1, 0, bank())
+        h_1 = hidden(1, parted_1)
+        gate(3)
+        scatter(0, 0, y_00)
+        scatter(1, 0, y_10)
+        quantise(1, h_1)
+        scatter(2, 0, message(2, 0, psum_a.tile([P, CH], F32, name="y_late", tag="a3")))
+        for nt, c in ((0, 1), (1, 1), (2, 1), (3, 0), (3, 1)):
+            scatter(nt, c, message(nt, c, bank()))

@@ -41,19 +41,25 @@ def tile_list_msg_tanh_res_gate_kernel(
         psum_a = ctx.enter_context(tc.psum_pool(name="psum_a", bufs=1))
         psum_y = ctx.enter_context(tc.psum_pool(name="psum_y", bufs=4))
 
+        w1_raw = []
+        for w, words in enumerate((ws_words, wt_words)):
+            raw = keep.tile([P, PASSES, R // 2], I32, name=f"w1_raw{w}", tag=f"g{w}", align_bytes=64)
+            nc.sync.dma_start(raw[:], words.rearrange("a p n -> p a n").bitcast(I32))
+            w1_raw.append(raw)
+
         src_list = keep.tile([P, LIST_COLS], U16, name="src_list")
         dst_list = keep.tile([P, LIST_COLS], U16, name="dst_list")
         nc.sync.dma_start(src_list[:], offs)
         nc.sync.dma_start(dst_list[:], offs2)
         lists = (src_list, dst_list)
 
-        tab_sc = keep.tile([P, T // 4], I32, name="tab_sc", align_bytes=64)
+        tab_sc = keep.tile([P, T // 4], I32, name="tab_sc", tag="tab_sc", align_bytes=64)
         nc.vector.memset(tab_sc[:], 0)
         for r in range(4):
             nc.sync.dma_start(
                 tab_sc[r:P:16, :], tab_scales.rearrange("a (q r) t -> r q a t", r=4)[r].bitcast(I32)
             )
-        w1_sc_raw = keep.tile([P, R // 4], I32, name="w1_sc_raw", tag="wd_sc", align_bytes=64)
+        w1_sc_raw = keep.tile([P, R // 4], I32, name="w1_sc_raw", tag="picked1", align_bytes=64)
         nc.vector.memset(w1_sc_raw[:], 0)
         for w, scales in enumerate((ws_scales, wt_scales)):
             for r in range(4):
@@ -61,22 +67,11 @@ def tile_list_msg_tanh_res_gate_kernel(
                     w1_sc_raw[8 * w + r : P : 16, :],
                     scales.rearrange("a (q r) n -> r q a n", r=4)[r].bitcast(I32),
                 )
-        w1_raw = []
-        for w, words in enumerate((ws_words, wt_words)):
-            raw = keep.tile([P, PASSES, R // 2], I32, name=f"w1_raw{w}", tag=f"g{w}", align_bytes=64)
-            nc.sync.dma_start(raw[:], words.rearrange("a p n -> p a n").bitcast(I32))
-            w1_raw.append(raw)
         table = keep.tile([P, T], I32, name="table", align_bytes=64)
         nc.sync.dma_start(table[:], tab_words[0].rearrange("p t b -> p (t b)").bitcast(I32))
 
-        sm_sb = keep.tile([P, PACK], F32, name="sm_sb")
-        nc.sync.dma_start(sm_sb[:], sm.rearrange("(p t) -> p t", t=PACK))
         wgo_sb = keep.tile([P, J], F32, name="wgo_sb")
         nc.sync.dma_start(wgo_sb[:], wgo)
-        wd4 = keep.tile([P, N // 2], I32, name="wd4", align_bytes=64)
-        wd8 = keep.tile([P, N], I32, name="wd8", align_bytes=64)
-        nc.sync.dma_start(wd4[:], wd4_words[0].bitcast(I32))
-        nc.sync.dma_start(wd8[:], wd8_words[0].rearrange("p n i -> p (n i)").bitcast(I32))
 
         v_moved = keep.tile([P, 2, J // 4], I32, name="v_moved", align_bytes=64)
         w_moved = keep.tile([P, 2 * PASSES - 1, R // 4], I32, name="w_moved", align_bytes=64)
@@ -87,13 +82,21 @@ def tile_list_msg_tanh_res_gate_kernel(
             count = P - max(rows_up, 16)
             nc.scalar.dma_start(moved[0:count, :], source[rows_up : rows_up + count, :])
 
-        v_sc = []
-        for s, lst in enumerate(lists):
-            picked = keep.tile([P, J // 4], I32, name=f"v_sc_picked{s}", align_bytes=64)
-            nc.vector.tensor_copy(picked[:].bitcast(U8), tab_sc[:].bitcast(U8).indirect(lst[:]))
-            shift(v_moved[:, s, :], picked, 16)
-            v_sc.append((picked[:], v_moved[:, s, :]))
 
+        w1 = keep.tile([P, 2 * PASSES, PACK, P], U16, name="w1", align_bytes=64)
+        for w in range(2):
+            nc.vector.tensor_copy(
+                w1[:, PASSES * w : PASSES * (w + 1), :, :],
+                w1_raw[w][:].bitcast(U16).rearrange("p a (m t) -> p a t m", t=PACK),
+            )
+
+        def look_up_scales(s):
+            picked = keep.tile([P, J // 4], I32, name=f"picked{s}", tag=f"picked{s}", align_bytes=64)
+            nc.vector.tensor_copy(picked[:].bitcast(U8), tab_sc[:].bitcast(U8).indirect(lists[s][:]))
+            shift(v_moved[:, s, :], picked, 16)
+            return picked[:], v_moved[:, s, :]
+
+        v_sc = [look_up_scales(0)]
         w1_sc_packed = keep.tile([P, R // 4], I32, name="w1_sc_packed", align_bytes=64)
         nc.vector.tensor_copy(
             w1_sc_packed[:].bitcast(U8).rearrange("p (t m) -> p t m", t=PACK),
@@ -103,22 +106,12 @@ def tile_list_msg_tanh_res_gate_kernel(
         for i in range(1, 2 * PASSES):
             shift(w_moved[:, i - 1, :], w1_sc_packed, 8 * (i // PASSES) + 16 * (i % PASSES))
             w1_sc.append(w_moved[:, i - 1, :])
-        w1 = keep.tile([P, 2 * PASSES, PACK, P], U16, name="w1", align_bytes=64)
-        for w in range(2):
-            nc.vector.tensor_copy(
-                w1[:, PASSES * w : PASSES * (w + 1), :, :],
-                w1_raw[w][:].bitcast(U16).rearrange("p a (m t) -> p a t m", t=PACK),
-            )
+        v_sc.append(look_up_scales(1))
 
-        wd_sc = keep.tile([P, 2, N // 4], I32, name="wd_sc", tag="wd_sc", align_bytes=64)
-        nc.vector.memset(wd_sc[:], 0)
-        for w, scales in enumerate((wd4_scales, wd8_scales)):
-            for q in range(QUADS):
-                nc.scalar.dma_start(
-                    wd_sc[32 * q : 32 * q + 4, w, :], scales[0, 4 * q : 4 * q + 4, :].bitcast(I32)
-                )
+        sm_sb = keep.tile([P, PACK], F32, name="sm_sb", tag="tab_sc", align_bytes=64)
+        nc.scalar.dma_start(sm_sb[:], sm.rearrange("(p t) -> p t", t=PACK))
 
-        gates = [keep.tile([P, J], F32, name=f"gate{nt}") for nt in range(N_TILES)]
+        gates = {}
 
         def look_up(c):
             picked_words = []
@@ -139,7 +132,7 @@ def tile_list_msg_tanh_res_gate_kernel(
 
         def hidden(c, parted):
             cols = slice(c * CH, (c + 1) * CH)
-            h_rows = ring.tile([P, PACK, CH], BF16, name="h_rows", align_bytes=64)
+            h_rows = keep.tile([P, PACK, CH], BF16, name=f"h_rows{c}", tag=f"h_rows{c}", align_bytes=64)
             for t in range(PACK):
                 acc = psum_a.tile([P, CH], F32, name="acc", tag=f"a{t}")
                 for i in range(2 * PASSES):
@@ -156,7 +149,7 @@ def tile_list_msg_tanh_res_gate_kernel(
                 th = ring.tile([P, CH], F32, name="th")
                 nc.scalar.activation(th[:], acc[:], TANH)
                 nc.scalar.activation(h_rows[:, t, :], th[:], COPY, scale=sm_sb[:, t : t + 1])
-            h_grouped = ring.tile([P, CH, PACK], BF16, name="h_grouped", align_bytes=64)
+            h_grouped = keep.tile([P, CH, PACK], BF16, name=f"h_grouped{c}", tag=("gate1", "h_grouped1")[c], align_bytes=64)
             nc.scalar.copy(h_grouped[:], h_rows[:].rearrange("p t j -> p j t"))
             return h_grouped
 
@@ -169,9 +162,11 @@ def tile_list_msg_tanh_res_gate_kernel(
             )
 
         def gate(nt):
-            nc.vector.tensor_tensor(gates[nt][:], g_sb[nt][:].indirect(src_list[:]), wgo_sb[:], MULT)
+            tile = keep.tile([P, J], F32, name=f"gate{nt}", tag=f"gate{nt}", align_bytes=64)
+            nc.vector.tensor_tensor(tile[:], g_sb[nt][:].indirect(src_list[:]), wgo_sb[:], MULT)
+            gates[nt] = tile
 
-        def message(nt, c, y):
+        def message(nt, c, y, y_sb):
             rows = slice(nt * P, (nt + 1) * P)
             cols = slice(c * CH, (c + 1) * CH)
             nc.tensor.matmul_mx(
@@ -192,22 +187,28 @@ def tile_list_msg_tanh_res_gate_kernel(
                 start=False,
                 stop=True,
             )
-            y_sb = msgs.tile([P, CH], F32, name="y_sb")
-            nc.scalar.copy(y_sb[:], y[:])
+            nc.scalar.copy(y_sb, y[:])
             return y_sb
 
-        def scatter(nt, c, y_sb):
+        def scatter(nt, first, last, y_sb):
+            window = windows[nt % WINDOWS]
             nc.vector.tensor_tensor(
-                windows[nt % WINDOWS][:].indirect(dst_list[:, c * CH_COLS : (c + 1) * CH_COLS]),
-                y_sb[:],
-                gates[nt][:, c * CH : (c + 1) * CH],
+                window[:].indirect(dst_list[:, first * CH_COLS : (last + 1) * CH_COLS]),
+                y_sb,
+                gates[nt][:, first * CH : (last + 1) * CH],
                 MULT,
             )
-            if c == CHUNKS - 1:
-                nc.sync.dma_start(out[nt * P : (nt + 1) * P, :], windows[nt % WINDOWS][:])
+            if last == CHUNKS - 1:
+                nc.sync.dma_start(out[nt * P : (nt + 1) * P, :], window[:])
 
         def bank():
             return psum_y.tile([P, CH], F32, name="y")
+
+        def hidden_bank(t):
+            return psum_a.tile([P, CH], F32, name="y_early", tag=f"a{t}")
+
+        def staging():
+            return msgs.tile([P, CH], F32, name="y_sb")[:]
 
         parted_0 = look_up(0)
         parted_1 = look_up(1)
@@ -216,26 +217,44 @@ def tile_list_msg_tanh_res_gate_kernel(
             g_tile = keep.tile([P, T], F32, name=f"g{nt}", tag=f"g{nt}", align_bytes=64)
             nc.sync.dma_start(g_tile[:], gT[nt * P : (nt + 1) * P, :])
             g_sb.append(g_tile)
+        wd_sc = keep.tile([P, 2, N // 4], I32, name="wd_sc", tag="g5", align_bytes=64)
+        nc.vector.memset(wd_sc[:], 0)
+        for w, scales in enumerate((wd4_scales, wd8_scales)):
+            for q in range(QUADS):
+                nc.sync.dma_start(
+                    wd_sc[32 * q : 32 * q + 4, w, :], scales[0, 4 * q : 4 * q + 4, :].bitcast(I32)
+                )
+        wd4 = keep.tile([P, N // 2], I32, name="wd4", align_bytes=64)
+        wd8 = keep.tile([P, N], I32, name="wd8", align_bytes=64)
+        nc.sync.dma_start(wd4[:], wd4_words[0].bitcast(I32))
+        nc.sync.dma_start(wd8[:], wd8_words[0].rearrange("p n i -> p (n i)").bitcast(I32))
         windows = [keep.tile([P, T], F32, name="window0")]
         nc.vector.memset(windows[0][:], 0.0)
+        warm = keep.tile([P, 1], F32, name="warm")
+        nc.scalar.activation(warm[:], windows[0][:, 0:1], TANH)
 
         h_0 = hidden(0, parted_0)
-        for nt in range(WINDOWS):
+        for nt in (0, 2):
             gate(nt)
-            if nt + 1 < WINDOWS:
-                window = keep.tile([P, T], F32, name=f"window{nt + 1}", tag=f"g{nt}", align_bytes=64)
-                nc.gpsimd.memset(window[:], 0.0)
-                windows.append(window)
-        h_codes = keep.tile([P, J], U32, name="h_codes", tag="g2", align_bytes=64)
+            window = keep.tile([P, T], F32, name=f"window{len(windows)}", tag=f"g{nt}", align_bytes=64)
+            nc.gpsimd.memset(window[:], 0.0)
+            windows.append(window)
+        gate(3)
+        h_codes = keep.tile([P, J], U32, name="h_codes", tag="g3", align_bytes=64)
         h_sc = keep.tile([P, J], U8, name="h_sc", align_bytes=64)
         quantise(0, h_0)
-        y_00 = message(0, 0, bank())
-        y_10 = message(1, 0, bank())
+        y_00 = message(0, 0, hidden_bank(3), staging())
+        y_10 = message(1, 0, bank(), staging())
         h_1 = hidden(1, parted_1)
-        gate(3)
-        scatter(0, 0, y_00)
-        scatter(1, 0, y_10)
+        gate(1)
+        scatter(0, 0, 0, y_00)
+        scatter(1, 0, 0, y_10)
         quantise(1, h_1)
-        scatter(2, 0, message(2, 0, psum_a.tile([P, CH], F32, name="y_late", tag="a3")))
-        for nt, c in ((0, 1), (1, 1), (2, 1), (3, 0), (3, 1)):
-            scatter(nt, c, message(nt, c, bank()))
+        y_20 = keep.tile([P, CH], F32, name="y_20", tag="h_rows1", align_bytes=64)
+        scatter(2, 0, 0, message(2, 0, bank(), y_20[:]))
+        for nt in range(WINDOWS):
+            scatter(nt, 1, 1, message(nt, 1, bank(), staging()))
+        y_last = keep.tile([P, J], F32, name="y_last")
+        for c in range(CHUNKS):
+            message(3, c, bank(), y_last[:, c * CH : (c + 1) * CH])
+        scatter(3, 0, 1, y_last[:])

@@ -1,6 +1,7 @@
 from contextlib import ExitStack
 
 import concourse.mybir as mybir
+from concourse.masks import make_identity
 
 K, R, N, T, J = 1024, 512, 512, 2048, 1024
 FLOPS = 2 * J * (2 * K * R + 2 * R * N)
@@ -26,7 +27,8 @@ CHUNKS = J // CH
 LIST_COLS = J // 16
 CH_COLS = CH // 16
 N_TILES = N // P
-WINDOWS = 3
+GROUP = 256
+PASS_ROWS = 16
 
 
 def tile_list_msg_tanh_res_gate_kernel(
@@ -36,145 +38,164 @@ def tile_list_msg_tanh_res_gate_kernel(
     nc = tc.nc
     with ExitStack() as ctx:
         keep = ctx.enter_context(tc.tile_pool(name="keep", bufs=1))
-        ring = ctx.enter_context(tc.tile_pool(name="ring", bufs=2))
-        msgs = ctx.enter_context(tc.tile_pool(name="msgs", bufs=4))
-        psum_a = ctx.enter_context(tc.psum_pool(name="psum_a", bufs=1))
-        psum_y = ctx.enter_context(tc.psum_pool(name="psum_y", bufs=4))
+        ring = ctx.enter_context(tc.tile_pool(name="ring", bufs=4))
+        msgs = ctx.enter_context(tc.tile_pool(name="msgs", bufs=3))
+        psum = ctx.enter_context(tc.psum_pool(name="psum", bufs=1))
 
-        w1_raw = []
-        for w, words in enumerate((ws_words, wt_words)):
-            raw = keep.tile([P, PASSES, R // 2], I32, name=f"w1_raw{w}", tag=f"g{w}", align_bytes=64)
-            nc.sync.dma_start(raw[:], words.rearrange("a p n -> p a n").bitcast(I32))
-            w1_raw.append(raw)
+        def held(name, shape, dtype, tag=None):
+            return keep.tile(shape, dtype, name=name, tag=tag or name, align_bytes=64)
 
         src_list = keep.tile([P, LIST_COLS], U16, name="src_list")
         dst_list = keep.tile([P, LIST_COLS], U16, name="dst_list")
-        nc.sync.dma_start(src_list[:], offs)
-        nc.sync.dma_start(dst_list[:], offs2)
         lists = (src_list, dst_list)
 
-        tab_sc = keep.tile([P, T // 4], I32, name="tab_sc", tag="tab_sc", align_bytes=64)
+        tab_sc = held("tab_sc", [P, T // 4], I32)
+        w1_sc = held("w1_sc", [P, 2 * PASSES, R // 4], I32)
+        moved = held("moved", [P, CHUNKS * 2, CH // 4], I32)
+        wd_sc = held("wd_sc", [P, 2, N // 4], I32)
+        windows = []
         nc.vector.memset(tab_sc[:], 0)
+        nc.vector.memset(w1_sc[:], 0)
+        nc.vector.memset(moved[:], 0)
+        nc.vector.memset(wd_sc[:], 0)
+
+        ident = held("ident", [P, P], F32)
+        make_identity(nc, ident[:])
+        warm = held("warm", [P, 1], F32)
+        nc.scalar.activation(warm[:], ident[:, 0:1], TANH)
+
+        nc.sync.dma_start(src_list[:], offs)
         for r in range(4):
             nc.sync.dma_start(
-                tab_sc[r:P:16, :], tab_scales.rearrange("a (q r) t -> r q a t", r=4)[r].bitcast(I32)
+                tab_sc[r:P:PASS_ROWS, :], tab_scales.rearrange("a (q r) t -> r q a t", r=4)[r].bitcast(I32)
             )
-        w1_sc_raw = keep.tile([P, R // 4], I32, name="w1_sc_raw", tag="picked1", align_bytes=64)
-        nc.vector.memset(w1_sc_raw[:], 0)
-        for w, scales in enumerate((ws_scales, wt_scales)):
-            for r in range(4):
-                nc.sync.dma_start(
-                    w1_sc_raw[8 * w + r : P : 16, :],
-                    scales.rearrange("a (q r) n -> r q a n", r=4)[r].bitcast(I32),
-                )
-        table = keep.tile([P, T], I32, name="table", align_bytes=64)
+        nc.sync.dma_start(dst_list[:], offs2)
+        table = held("table", [P, T], I32)
         nc.sync.dma_start(table[:], tab_words[0].rearrange("p t b -> p (t b)").bitcast(I32))
 
-        wgo_sb = keep.tile([P, J], F32, name="wgo_sb")
-        nc.sync.dma_start(wgo_sb[:], wgo)
-
-        v_moved = keep.tile([P, 2, J // 4], I32, name="v_moved", align_bytes=64)
-        w_moved = keep.tile([P, 2 * PASSES - 1, R // 4], I32, name="w_moved", align_bytes=64)
-        nc.vector.memset(v_moved[:], 0)
-        nc.vector.memset(w_moved[:], 0)
-
-        def shift(moved, source, rows_up):
-            count = P - max(rows_up, 16)
-            nc.scalar.dma_start(moved[0:count, :], source[rows_up : rows_up + count, :])
-
-
-        w1 = keep.tile([P, 2 * PASSES, PACK, P], U16, name="w1", align_bytes=64)
-        for w in range(2):
-            nc.vector.tensor_copy(
-                w1[:, PASSES * w : PASSES * (w + 1), :, :],
-                w1_raw[w][:].bitcast(U16).rearrange("p a (m t) -> p a t m", t=PACK),
+        def load_w1_scales(w, r):
+            scales = (ws_scales, wt_scales)[w]
+            nc.sync.dma_start(
+                w1_sc[r:P:32, PASSES * w : PASSES * (w + 1), :],
+                scales.rearrange("a (q r) n -> r q a n", r=4)[r].bitcast(I32),
             )
 
-        def look_up_scales(s):
-            picked = keep.tile([P, J // 4], I32, name=f"picked{s}", tag=f"picked{s}", align_bytes=64)
-            nc.vector.tensor_copy(picked[:].bitcast(U8), tab_sc[:].bitcast(U8).indirect(lists[s][:]))
-            shift(v_moved[:, s, :], picked, 16)
-            return picked[:], v_moved[:, s, :]
+        def load_w1_words(w):
+            words = held(f"w1_words{w}", [P, PASSES, R // 2], I32)
+            nc.sync.dma_start(words[:], (ws_words, wt_words)[w].rearrange("a p n -> p a n").bitcast(I32))
+            return words
 
-        v_sc = [look_up_scales(0)]
-        w1_sc_packed = keep.tile([P, R // 4], I32, name="w1_sc_packed", align_bytes=64)
-        nc.vector.tensor_copy(
-            w1_sc_packed[:].bitcast(U8).rearrange("p (t m) -> p t m", t=PACK),
-            w1_sc_raw[:].bitcast(U8).rearrange("p (m t) -> p t m", t=PACK),
-        )
-        w1_sc = [w1_sc_packed[:]]
-        for i in range(1, 2 * PASSES):
-            shift(w_moved[:, i - 1, :], w1_sc_packed, 8 * (i // PASSES) + 16 * (i % PASSES))
-            w1_sc.append(w_moved[:, i - 1, :])
-        v_sc.append(look_up_scales(1))
+        def load_wd_scales(w, q):
+            scales = (wd4_scales, wd8_scales)[w]
+            nc.sync.dma_start(wd_sc[32 * q : 32 * q + 4, w, :], scales[0, 4 * q : 4 * q + 4, :].bitcast(I32))
 
-        sm_sb = keep.tile([P, PACK], F32, name="sm_sb", tag="tab_sc", align_bytes=64)
-        nc.scalar.dma_start(sm_sb[:], sm.rearrange("(p t) -> p t", t=PACK))
+        def load_gate_rows(nt):
+            rows = held(f"g{nt}", [P, T], F32)
+            nc.sync.dma_start(rows[:], gT[nt * P : (nt + 1) * P, :])
+            return rows
 
-        gates = {}
+        w1_scale_loads = [(w, r) for w in range(2) for r in range(4)]
+        for w, r in w1_scale_loads[:7]:
+            load_w1_scales(w, r)
+        w1_words = [load_w1_words(0)]
+        load_w1_scales(*w1_scale_loads[7])
+        w1_words.append(load_w1_words(1))
 
-        def look_up(c):
-            picked_words = []
-            for s, lst in enumerate(lists):
-                both = keep.tile([P, CH], U32, name=f"both{c}{s}", tag=f"g{2 + 2 * c + s}", align_bytes=64)
+        def look_up_scales(c):
+            picked = []
+            for s in range(2):
+                tag = f"picked{s}" if c == 0 else f"both0{s}"
+                tile = held(f"picked{c}{s}", [P, CH // 4], I32, tag=tag)
                 nc.vector.tensor_copy(
-                    both[:], table[:].bitcast(U32).indirect(lst[:, c * CH_COLS : (c + 1) * CH_COLS])
+                    tile[:].bitcast(U8),
+                    tab_sc[:].bitcast(U8).indirect(lists[s][:, c * CH_COLS : (c + 1) * CH_COLS]),
                 )
-                picked_words.append(both)
+                picked.append(tile)
+            return picked
+
+        def move_scales(c, picked):
+            planes = []
+            for s in range(2):
+                down = moved[:, 2 * c + s, :]
+                nc.sync.dma_start(moved[0 : P - PASS_ROWS, 2 * c + s, :], picked[s][PASS_ROWS:P, :])
+                planes.append((picked[s][:], down))
+            return planes
+
+        def look_up_words(c):
+            both = []
+            for s in range(2):
+                tile = held(f"both{c}{s}", [P, CH], U32)
+                nc.vector.tensor_copy(
+                    tile[:], table[:].bitcast(U32).indirect(lists[s][:, c * CH_COLS : (c + 1) * CH_COLS])
+                )
+                both.append(tile)
             parted = []
             for s in range(2):
-                apart = ring.tile([P, PASSES, CH], U16, name=f"apart{s}", align_bytes=64)
+                apart = held(f"apart{c}{s}", [P, PASSES, CH], U16)
                 nc.vector.tensor_copy(
-                    apart[:], picked_words[s][:].bitcast(U16).rearrange("p (j d) -> p d j", d=PASSES)
+                    apart[:], both[s][:].bitcast(U16).rearrange("p (j d) -> p d j", d=PASSES)
                 )
                 parted.append(apart)
             return parted
 
-        def hidden(c, parted):
-            cols = slice(c * CH, (c + 1) * CH)
-            h_rows = keep.tile([P, PACK, CH], BF16, name=f"h_rows{c}", tag=f"h_rows{c}", align_bytes=64)
-            for t in range(PACK):
-                acc = psum_a.tile([P, CH], F32, name="acc", tag=f"a{t}")
-                for i in range(2 * PASSES):
-                    s, a = divmod(i, PASSES)
-                    nc.tensor.matmul_mx(
-                        out=acc[:],
-                        lhsT=w1[:, i, t, :].bitcast(FP4X4),
-                        lhsT_scale=w1_sc[i].bitcast(U8)[:, t * P : (t + 1) * P],
-                        rhs=parted[s][:, a, :].bitcast(FP4X4),
-                        rhs_scale=v_sc[s][a].bitcast(U8)[:, cols],
-                        start=(i == 0),
-                        stop=(i == 2 * PASSES - 1),
-                    )
-                th = ring.tile([P, CH], F32, name="th")
-                nc.scalar.activation(th[:], acc[:], TANH)
-                nc.scalar.activation(h_rows[:, t, :], th[:], COPY, scale=sm_sb[:, t : t + 1])
-            h_grouped = keep.tile([P, CH, PACK], BF16, name=f"h_grouped{c}", tag=("gate1", "h_grouped1")[c], align_bytes=64)
-            nc.scalar.copy(h_grouped[:], h_rows[:].rearrange("p t j -> p j t"))
-            return h_grouped
+        def first_layer(jt, parted, planes):
+            cols = slice((jt % 4) * P, (jt % 4 + 1) * P)
+            acc = psum.tile([P, R], F32, name=f"acc{jt}", tag=f"a{jt % 4}")
+            for i in range(2 * PASSES):
+                a, s = divmod(i if jt == 0 else 2 * PASSES - 1 - i, 2)
+                nc.tensor.matmul_mx(
+                    out=acc[:],
+                    lhsT=parted[s][:, a, cols].bitcast(FP4X4),
+                    lhsT_scale=planes[s][a].bitcast(U8)[:, cols],
+                    rhs=w1_words[s][:, a, :].bitcast(FP4X4),
+                    rhs_scale=w1_sc[:, PASSES * s + a, :].bitcast(U8),
+                    start=(i == 0),
+                    stop=(i == 2 * PASSES - 1),
+                )
+            th = ring.tile([P, PACK, P], F32, name="th")
+            nc.scalar.activation(th[:], acc[:].rearrange("j (m t) -> j t m", t=PACK), TANH)
+            return th
 
-        def quantise(c, h_grouped):
-            cols = slice(c * CH, (c + 1) * CH)
+        def turn(g, half, th, banks):
+            for t in range(PACK):
+                nc.tensor.transpose(banks[t // 2][:, t % 2, half * P : (half + 1) * P], th[:, t, :], ident[:])
+
+        def hidden(g, ths, h_grouped):
+            banks = [
+                psum.tile([P, 2, GROUP], F32, name=f"turned{g}{u}", tag=f"t{2 * (g % 2) + u}") for u in range(2)
+            ]
+            for half in range(2):
+                turn(g, half, ths[half], banks)
+            h_rows = held(f"h_rows{g}", [P, PACK, GROUP], BF16)
+            for t in range(PACK):
+                nc.scalar.activation(h_rows[:, t, :], banks[t // 2][:, t % 2, :], COPY, scale=sm_sb[:, t : t + 1])
+            cols = slice((g % 2) * GROUP, (g % 2 + 1) * GROUP)
+            nc.scalar.copy(h_grouped[:, cols, :], h_rows[:].rearrange("p t j -> p j t"))
+
+        def quantise(c, h_grouped, tag):
+            codes = held(f"h_codes{c}", [P, CH], U32, tag=tag)
+            scales = held(f"h_sc{c}", [P, CH], U8)
             nc.vector.quantize_mx(
-                out=h_codes[:, cols].bitcast(FP8X4),
-                scales=h_sc[:, cols],
+                out=codes[:].bitcast(FP8X4),
+                scales=scales[:],
                 in_=h_grouped[:].rearrange("p j t -> p (j t)"),
             )
+            return codes, scales
 
         def gate(nt):
-            tile = keep.tile([P, J], F32, name=f"gate{nt}", tag=f"gate{nt}", align_bytes=64)
+            tile = held(f"gate{nt}", [P, J], F32)
             nc.vector.tensor_tensor(tile[:], g_sb[nt][:].indirect(src_list[:]), wgo_sb[:], MULT)
-            gates[nt] = tile
+            return tile
 
-        def message(nt, c, y, y_sb):
+        def message(nt, h, y, y_sb):
             rows = slice(nt * P, (nt + 1) * P)
-            cols = slice(c * CH, (c + 1) * CH)
+            codes, scales = h
             nc.tensor.matmul_mx(
                 out=y[:],
                 lhsT=wd4[:, nt * P // 2 : (nt + 1) * P // 2].bitcast(FP4X4),
                 lhsT_scale=wd_sc[:, 0, :].bitcast(U8)[:, rows],
-                rhs=h_codes[:, cols].bitcast(FP8X4),
-                rhs_scale=h_sc[:, cols],
+                rhs=codes[:].bitcast(FP8X4),
+                rhs_scale=scales[:],
                 start=True,
                 stop=False,
             )
@@ -182,8 +203,8 @@ def tile_list_msg_tanh_res_gate_kernel(
                 out=y[:],
                 lhsT=wd8[:, rows].bitcast(FP8X4),
                 lhsT_scale=wd_sc[:, 1, :].bitcast(U8)[:, rows],
-                rhs=h_codes[:, cols].bitcast(FP8X4),
-                rhs_scale=h_sc[:, cols],
+                rhs=codes[:].bitcast(FP8X4),
+                rhs_scale=scales[:],
                 start=False,
                 stop=True,
             )
@@ -191,7 +212,7 @@ def tile_list_msg_tanh_res_gate_kernel(
             return y_sb
 
         def scatter(nt, first, last, y_sb):
-            window = windows[nt % WINDOWS]
+            window = windows[nt % len(windows)]
             nc.vector.tensor_tensor(
                 window[:].indirect(dst_list[:, first * CH_COLS : (last + 1) * CH_COLS]),
                 y_sb,
@@ -201,60 +222,70 @@ def tile_list_msg_tanh_res_gate_kernel(
             if last == CHUNKS - 1:
                 nc.sync.dma_start(out[nt * P : (nt + 1) * P, :], window[:])
 
-        def bank():
-            return psum_y.tile([P, CH], F32, name="y")
-
-        def hidden_bank(t):
-            return psum_a.tile([P, CH], F32, name="y_early", tag=f"a{t}")
+        def bank(tag):
+            return psum.tile([P, CH], F32, name=f"y_{tag}", tag=tag)
 
         def staging():
             return msgs.tile([P, CH], F32, name="y_sb")[:]
 
-        parted_0 = look_up(0)
-        parted_1 = look_up(1)
-        g_sb = []
-        for nt in range(N_TILES):
-            g_tile = keep.tile([P, T], F32, name=f"g{nt}", tag=f"g{nt}", align_bytes=64)
-            nc.sync.dma_start(g_tile[:], gT[nt * P : (nt + 1) * P, :])
-            g_sb.append(g_tile)
-        wd_sc = keep.tile([P, 2, N // 4], I32, name="wd_sc", tag="g5", align_bytes=64)
-        nc.vector.memset(wd_sc[:], 0)
-        for w, scales in enumerate((wd4_scales, wd8_scales)):
-            for q in range(QUADS):
-                nc.sync.dma_start(
-                    wd_sc[32 * q : 32 * q + 4, w, :], scales[0, 4 * q : 4 * q + 4, :].bitcast(I32)
-                )
-        wd4 = keep.tile([P, N // 2], I32, name="wd4", align_bytes=64)
-        wd8 = keep.tile([P, N], I32, name="wd8", align_bytes=64)
-        nc.sync.dma_start(wd4[:], wd4_words[0].bitcast(I32))
-        nc.sync.dma_start(wd8[:], wd8_words[0].rearrange("p n i -> p (n i)").bitcast(I32))
-        windows = [keep.tile([P, T], F32, name="window0")]
-        nc.vector.memset(windows[0][:], 0.0)
-        warm = keep.tile([P, 1], F32, name="warm")
-        nc.scalar.activation(warm[:], windows[0][:, 0:1], TANH)
-
-        h_0 = hidden(0, parted_0)
-        for nt in (0, 2):
-            gate(nt)
-            window = keep.tile([P, T], F32, name=f"window{len(windows)}", tag=f"g{nt}", align_bytes=64)
+        def new_window(tag):
+            window = held(f"window{len(windows)}", [P, T], F32, tag=tag)
             nc.gpsimd.memset(window[:], 0.0)
             windows.append(window)
-        gate(3)
-        h_codes = keep.tile([P, J], U32, name="h_codes", tag="g3", align_bytes=64)
-        h_sc = keep.tile([P, J], U8, name="h_sc", align_bytes=64)
-        quantise(0, h_0)
-        y_00 = message(0, 0, hidden_bank(3), staging())
-        y_10 = message(1, 0, bank(), staging())
-        h_1 = hidden(1, parted_1)
-        gate(1)
-        scatter(0, 0, 0, y_00)
+
+        picked_0 = look_up_scales(0)
+        planes_0 = move_scales(0, picked_0)
+        parted_0 = look_up_words(0)
+
+        sm_sb = held("sm_sb", [P, PACK], F32)
+        nc.sync.dma_start(sm_sb[:], sm.rearrange("(p t) -> p t", t=PACK))
+        wd_scale_loads = [(w, q) for w in range(2) for q in range(QUADS)]
+        for w, q in wd_scale_loads[:2]:
+            load_wd_scales(w, q)
+        wgo_sb = held("wgo_sb", [P, J], F32)
+        nc.sync.dma_start(wgo_sb[:], wgo)
+        g_sb = [load_gate_rows(0)]
+        for w, q in wd_scale_loads[2:]:
+            load_wd_scales(w, q)
+        g_sb.append(load_gate_rows(1))
+
+        picked_1 = look_up_scales(1)
+        planes_1 = move_scales(1, picked_1)
+        parted_1 = look_up_words(1)
+
+        g_sb.append(load_gate_rows(2))
+        wd8 = held("wd8", [P, N], I32)
+        nc.sync.dma_start(wd8[:], wd8_words[0].rearrange("p n i -> p (n i)").bitcast(I32))
+        g_sb.append(load_gate_rows(3))
+        wd4 = held("wd4", [P, N // 2], I32)
+        nc.sync.dma_start(wd4[:], wd4_words[0].bitcast(I32))
+
+        h_grouped_0 = held("h_grouped0", [P, CH, PACK], BF16)
+        h_grouped_1 = held("h_grouped1", [P, CH, PACK], BF16)
+        for g in range(2):
+            hidden(g, [first_layer(2 * g + half, parted_0, planes_0) for half in range(2)], h_grouped_0)
+        gates = [gate(0)]
+        new_window("g0")
+        gates.append(gate(1))
+        gates.append(gate(2))
+        ths = [first_layer(jt, parted_1, planes_1) for jt in range(4, 8)]
+        h_0 = quantise(0, h_grouped_0, "g2")
+        y_00 = held("y_00", [P, CH], F32)
+        message(0, h_0, bank("t0"), y_00[:])
+        y_10 = message(1, h_0, bank("t2"), staging())
+        for g in range(2, 4):
+            hidden(g, ths[2 * g - 4 : 2 * g - 2], h_grouped_1)
+        gates.append(gate(3))
+        new_window("g3")
+        new_window("wgo_sb")
+        scatter(0, 0, 0, y_00[:])
         scatter(1, 0, 0, y_10)
-        quantise(1, h_1)
-        y_20 = keep.tile([P, CH], F32, name="y_20", tag="h_rows1", align_bytes=64)
-        scatter(2, 0, 0, message(2, 0, bank(), y_20[:]))
-        for nt in range(WINDOWS):
-            scatter(nt, 1, 1, message(nt, 1, bank(), staging()))
-        y_last = keep.tile([P, J], F32, name="y_last")
-        for c in range(CHUNKS):
-            message(3, c, bank(), y_last[:, c * CH : (c + 1) * CH])
+        h_1 = quantise(1, h_grouped_1, "y_00")
+        y_20 = held("y_20", [P, CH], F32, tag="h_rows3")
+        scatter(2, 0, 0, message(2, h_0, bank("a0"), y_20[:]))
+        for nt in range(len(windows)):
+            scatter(nt, 1, 1, message(nt, h_1, bank(f"a{nt + 1}"), staging()))
+        y_last = held("y_last", [P, J], F32)
+        for c, h in enumerate((h_0, h_1)):
+            message(3, h, bank(f"t{c}"), y_last[:, c * CH : (c + 1) * CH])
         scatter(3, 0, 1, y_last[:])

@@ -29,6 +29,7 @@ CH_COLS = CH // 16
 N_TILES = N // P
 GROUP = 256
 PASS_ROWS = 16
+WINDOWS = 3
 
 
 def tile_list_msg_tanh_res_gate_kernel(
@@ -40,9 +41,12 @@ def tile_list_msg_tanh_res_gate_kernel(
         keep = ctx.enter_context(tc.tile_pool(name="keep", bufs=1))
         ring = ctx.enter_context(tc.tile_pool(name="ring", bufs=4))
         msgs = ctx.enter_context(tc.tile_pool(name="msgs", bufs=3))
+        shared = ctx.enter_context(tc.tile_pool(name="shared", bufs=1))
         psum = ctx.enter_context(tc.psum_pool(name="psum", bufs=1))
 
-        def held(name, shape, dtype, tag=None):
+        def held(name, shape, dtype, tag=None, offset=None):
+            if offset is not None:
+                return shared.tile(shape, dtype, name=name, align_bytes=64, offset=offset)
             return keep.tile(shape, dtype, name=name, tag=tag or name, align_bytes=64)
 
         src_list = keep.tile([P, LIST_COLS], U16, name="src_list")
@@ -53,11 +57,12 @@ def tile_list_msg_tanh_res_gate_kernel(
         w1_sc = held("w1_sc", [P, 2 * PASSES, R // 4], I32)
         moved = held("moved", [P, CHUNKS * 2, CH // 4], I32)
         wd_sc = held("wd_sc", [P, 2, N // 4], I32)
-        windows = []
+        windows = [held("window0", [P, T], F32)]
         nc.vector.memset(tab_sc[:], 0)
         nc.vector.memset(w1_sc[:], 0)
         nc.vector.memset(moved[:], 0)
         nc.vector.memset(wd_sc[:], 0)
+        nc.vector.memset(windows[0][:], 0.0)
 
         ident = held("ident", [P, P], F32)
         make_identity(nc, ident[:])
@@ -90,7 +95,7 @@ def tile_list_msg_tanh_res_gate_kernel(
             nc.sync.dma_start(wd_sc[32 * q : 32 * q + 4, w, :], scales[0, 4 * q : 4 * q + 4, :].bitcast(I32))
 
         def load_gate_rows(nt):
-            rows = held(f"g{nt}", [P, T], F32)
+            rows = held(f"g{nt}", [P, T], F32, offset=0 if nt == 1 else None)
             nc.sync.dma_start(rows[:], gT[nt * P : (nt + 1) * P, :])
             return rows
 
@@ -169,12 +174,11 @@ def tile_list_msg_tanh_res_gate_kernel(
             h_rows = held(f"h_rows{g}", [P, PACK, GROUP], BF16)
             for t in range(PACK):
                 nc.scalar.activation(h_rows[:, t, :], banks[t // 2][:, t % 2, :], COPY, scale=sm_sb[:, t : t + 1])
-            cols = slice((g % 2) * GROUP, (g % 2 + 1) * GROUP)
-            nc.scalar.copy(h_grouped[:, cols, :], h_rows[:].rearrange("p t j -> p j t"))
+            nc.scalar.copy(h_grouped, h_rows[:].rearrange("p t j -> p j t"))
 
-        def quantise(c, h_grouped, tag):
-            codes = held(f"h_codes{c}", [P, CH], U32, tag=tag)
-            scales = held(f"h_sc{c}", [P, CH], U8)
+        def quantise(name, h_grouped, width, tag=None, offset=None):
+            codes = held(f"h_codes{name}", [P, width], U32, tag=tag, offset=offset)
+            scales = held(f"h_sc{name}", [P, width], U8)
             nc.vector.quantize_mx(
                 out=codes[:].bitcast(FP8X4),
                 scales=scales[:],
@@ -182,44 +186,53 @@ def tile_list_msg_tanh_res_gate_kernel(
             )
             return codes, scales
 
-        def gate(nt):
-            tile = held(f"gate{nt}", [P, J], F32)
-            nc.vector.tensor_tensor(tile[:], g_sb[nt][:].indirect(src_list[:]), wgo_sb[:], MULT)
-            return tile
+        def gate(nt, first, count, offset=None):
+            tile = held(f"gate{nt}_{first}", [P, count], F32, offset=offset)
+            nc.vector.tensor_tensor(
+                tile[:],
+                g_sb[nt][:].indirect(src_list[:, first // 16 : (first + count) // 16]),
+                wgo_sb[:, first : first + count],
+                MULT,
+            )
+            gates[nt, first] = tile
 
-        def message(nt, h, y, y_sb):
+        def second_layer(nt, h, cols, y):
             rows = slice(nt * P, (nt + 1) * P)
             codes, scales = h
             nc.tensor.matmul_mx(
-                out=y[:],
+                out=y,
                 lhsT=wd4[:, nt * P // 2 : (nt + 1) * P // 2].bitcast(FP4X4),
                 lhsT_scale=wd_sc[:, 0, :].bitcast(U8)[:, rows],
-                rhs=codes[:].bitcast(FP8X4),
-                rhs_scale=scales[:],
+                rhs=codes[:, cols].bitcast(FP8X4),
+                rhs_scale=scales[:, cols],
                 start=True,
                 stop=False,
             )
             nc.tensor.matmul_mx(
-                out=y[:],
+                out=y,
                 lhsT=wd8[:, rows].bitcast(FP8X4),
                 lhsT_scale=wd_sc[:, 1, :].bitcast(U8)[:, rows],
-                rhs=codes[:].bitcast(FP8X4),
-                rhs_scale=scales[:],
+                rhs=codes[:, cols].bitcast(FP8X4),
+                rhs_scale=scales[:, cols],
                 start=False,
                 stop=True,
             )
+
+        def message(nt, h, y, y_sb):
+            second_layer(nt, h, slice(0, CH), y[:])
             nc.scalar.copy(y_sb, y[:])
             return y_sb
 
-        def scatter(nt, first, last, y_sb):
-            window = windows[nt % len(windows)]
+        def scatter(nt, first, y_sb, gate_values):
+            count = y_sb.shape[1]
+            window = windows[nt % WINDOWS]
             nc.vector.tensor_tensor(
-                window[:].indirect(dst_list[:, first * CH_COLS : (last + 1) * CH_COLS]),
+                window[:].indirect(dst_list[:, first // 16 : (first + count) // 16]),
                 y_sb,
-                gates[nt][:, first * CH : (last + 1) * CH],
+                gate_values,
                 MULT,
             )
-            if last == CHUNKS - 1:
+            if first + count == J:
                 nc.sync.dma_start(out[nt * P : (nt + 1) * P, :], window[:])
 
         def bank(tag):
@@ -239,53 +252,54 @@ def tile_list_msg_tanh_res_gate_kernel(
 
         sm_sb = held("sm_sb", [P, PACK], F32)
         nc.sync.dma_start(sm_sb[:], sm.rearrange("(p t) -> p t", t=PACK))
-        wd_scale_loads = [(w, q) for w in range(2) for q in range(QUADS)]
-        for w, q in wd_scale_loads[:2]:
-            load_wd_scales(w, q)
         wgo_sb = held("wgo_sb", [P, J], F32)
         nc.sync.dma_start(wgo_sb[:], wgo)
-        g_sb = [load_gate_rows(0)]
-        for w, q in wd_scale_loads[2:]:
-            load_wd_scales(w, q)
-        g_sb.append(load_gate_rows(1))
+        g_sb = {nt: load_gate_rows(nt) for nt in (0, 2)}
+        for q in range(QUADS):
+            load_wd_scales(0, q)
 
         picked_1 = look_up_scales(1)
         planes_1 = move_scales(1, picked_1)
         parted_1 = look_up_words(1)
 
-        g_sb.append(load_gate_rows(2))
+        for nt in (1, 3):
+            g_sb[nt] = load_gate_rows(nt)
+        for q in range(QUADS):
+            load_wd_scales(1, q)
         wd8 = held("wd8", [P, N], I32)
         nc.sync.dma_start(wd8[:], wd8_words[0].rearrange("p n i -> p (n i)").bitcast(I32))
-        g_sb.append(load_gate_rows(3))
         wd4 = held("wd4", [P, N // 2], I32)
         nc.sync.dma_start(wd4[:], wd4_words[0].bitcast(I32))
 
-        h_grouped_0 = held("h_grouped0", [P, CH, PACK], BF16)
-        h_grouped_1 = held("h_grouped1", [P, CH, PACK], BF16)
+        grouped = [held(f"h_grouped{c}", [P, CH, PACK], BF16) for c in range(CHUNKS)]
+        halves = (slice(0, GROUP), slice(GROUP, CH))
+        ths = [first_layer(jt, parted_0, planes_0) for jt in range(4)]
         for g in range(2):
-            hidden(g, [first_layer(2 * g + half, parted_0, planes_0) for half in range(2)], h_grouped_0)
-        gates = [gate(0)]
+            hidden(g, ths[2 * g : 2 * g + 2], grouped[0][:, halves[g], :])
+        ths_late = [first_layer(jt, parted_1, planes_1) for jt in range(4, 8)]
+        gates = {}
+        gate(0, 0, J)
         new_window("g0")
-        gates.append(gate(1))
-        gates.append(gate(2))
-        ths = [first_layer(jt, parted_1, planes_1) for jt in range(4, 8)]
-        h_0 = quantise(0, h_grouped_0, "g2")
-        y_00 = held("y_00", [P, CH], F32)
-        message(0, h_0, bank("t0"), y_00[:])
-        y_10 = message(1, h_0, bank("t2"), staging())
-        for g in range(2, 4):
-            hidden(g, ths[2 * g - 4 : 2 * g - 2], h_grouped_1)
-        gates.append(gate(3))
-        new_window("g3")
-        new_window("wgo_sb")
-        scatter(0, 0, 0, y_00[:])
-        scatter(1, 0, 0, y_10)
-        h_1 = quantise(1, h_grouped_1, "y_00")
-        y_20 = held("y_20", [P, CH], F32, tag="h_rows3")
-        scatter(2, 0, 0, message(2, h_0, bank("a0"), y_20[:]))
-        for nt in range(len(windows)):
-            scatter(nt, 1, 1, message(nt, h_1, bank(f"a{nt + 1}"), staging()))
+        gate(2, 0, CH)
+        gate(1, 0, J)
+        h_0 = quantise("0", grouped[0], CH, offset=0)
+        new_window("h_grouped0")
+        gate(2, CH, CH, offset=4 * CH)
+        gate(3, 0, J)
+        early = [held(f"y_early{nt}", [P, CH], F32) for nt in range(2)]
+        for nt, tag in enumerate(("t0", "t2")):
+            message(nt, h_0, bank(tag), early[nt][:])
+        for g in range(2):
+            hidden(2 + g, ths_late[2 * g : 2 * g + 2], grouped[1][:, halves[g], :])
+        for nt in range(2):
+            scatter(nt, 0, early[nt][:], gates[nt, 0][:, 0:CH])
+        h_1 = quantise("1", grouped[1], CH, "y_early0")
+        y_2 = held("y_2", [P, CH], F32, tag="h_rows3")
+        scatter(2, 0, message(2, h_0, bank("a0"), y_2[:]), gates[2, 0][:])
+        late_gates = (gates[0, 0][:, CH:J], gates[1, 0][:, CH:J], gates[2, CH][:])
+        for nt in range(WINDOWS):
+            scatter(nt, CH, message(nt, h_1, bank(f"a{nt + 1}"), staging()), late_gates[nt])
         y_last = held("y_last", [P, J], F32)
         for c, h in enumerate((h_0, h_1)):
             message(3, h, bank(f"t{c}"), y_last[:, c * CH : (c + 1) * CH])
-        scatter(3, 0, 1, y_last[:])
+        scatter(3, 0, y_last[:], gates[3, 0][:])

@@ -57,17 +57,14 @@ def tile_list_msg_tanh_res_gate_kernel(
         w1_sc = held("w1_sc", [P, 2 * PASSES, R // 4], I32)
         moved = held("moved", [P, CHUNKS * 2, CH // 4], I32)
         wd_sc = held("wd_sc", [P, 2, N // 4], I32)
-        windows = [held("window0", [P, T], F32)]
+        windows = []
         nc.vector.memset(tab_sc[:], 0)
         nc.vector.memset(w1_sc[:], 0)
         nc.vector.memset(moved[:], 0)
         nc.vector.memset(wd_sc[:], 0)
-        nc.vector.memset(windows[0][:], 0.0)
 
         ident = held("ident", [P, P], F32)
         make_identity(nc, ident[:])
-        warm = held("warm", [P, 1], F32)
-        nc.scalar.activation(warm[:], ident[:, 0:1], TANH)
 
         nc.sync.dma_start(src_list[:], offs)
         for r in range(4):
@@ -285,6 +282,7 @@ def tile_list_msg_tanh_res_gate_kernel(
         h_0 = quantise("0", grouped[0], CH, offset=0)
         new_window("h_grouped0")
         gate(2, CH, CH, offset=4 * CH)
+        new_window("g2")
         gate(3, 0, J)
         early = [held(f"y_early{nt}", [P, CH], F32) for nt in range(2)]
         for nt, tag in enumerate(("t0", "t2")):

@@ -29,6 +29,7 @@ CH_COLS = CH // 16
 N_TILES = N // P
 GROUP = 256
 PASS_ROWS = 16
+SCALE_BASE = 96
 WINDOWS = 3
 
 
@@ -39,7 +40,6 @@ def tile_list_msg_tanh_res_gate_kernel(
     nc = tc.nc
     with ExitStack() as ctx:
         keep = ctx.enter_context(tc.tile_pool(name="keep", bufs=1))
-        ring = ctx.enter_context(tc.tile_pool(name="ring", bufs=4))
         msgs = ctx.enter_context(tc.tile_pool(name="msgs", bufs=3))
         shared = ctx.enter_context(tc.tile_pool(name="shared", bufs=1))
         psum = ctx.enter_context(tc.psum_pool(name="psum", bufs=1))
@@ -55,22 +55,19 @@ def tile_list_msg_tanh_res_gate_kernel(
 
         tab_sc = held("tab_sc", [P, T // 4], I32)
         w1_sc = held("w1_sc", [P, 2 * PASSES, R // 4], I32)
-        moved = held("moved", [P, CHUNKS * 2, CH // 4], I32)
+        planes = held("planes", [P, PASSES, 2, J // 4], I32)
         wd_sc = held("wd_sc", [P, 2, N // 4], I32)
         windows = []
-        nc.vector.memset(tab_sc[:], 0)
         nc.vector.memset(w1_sc[:], 0)
-        nc.vector.memset(moved[:], 0)
-        nc.vector.memset(wd_sc[:], 0)
+        nc.vector.memset(tab_sc[0:SCALE_BASE, :], 0)
 
         ident = held("ident", [P, P], F32)
         make_identity(nc, ident[:])
+        nc.gpsimd.memset(planes[:], 0)
+        nc.gpsimd.memset(wd_sc[:], 0)
 
         nc.sync.dma_start(src_list[:], offs)
-        for r in range(4):
-            nc.sync.dma_start(
-                tab_sc[r:P:PASS_ROWS, :], tab_scales.rearrange("a (q r) t -> r q a t", r=4)[r].bitcast(I32)
-            )
+        nc.sync.dma_start(tab_sc[SCALE_BASE:P, :], tab_scales.rearrange("a q t -> (a q) t").bitcast(I32))
         nc.sync.dma_start(dst_list[:], offs2)
         table = held("table", [P, T], I32)
         nc.sync.dma_start(table[:], tab_words[0].rearrange("p t b -> p (t b)").bitcast(I32))
@@ -92,36 +89,26 @@ def tile_list_msg_tanh_res_gate_kernel(
             nc.sync.dma_start(wd_sc[32 * q : 32 * q + 4, w, :], scales[0, 4 * q : 4 * q + 4, :].bitcast(I32))
 
         def load_gate_rows(nt):
-            rows = held(f"g{nt}", [P, T], F32, offset=0 if nt == 1 else None)
+            rows = held(f"g{nt}", [P, T], F32, offset=None)
             nc.sync.dma_start(rows[:], gT[nt * P : (nt + 1) * P, :])
             return rows
 
-        w1_scale_loads = [(w, r) for w in range(2) for r in range(4)]
-        for w, r in w1_scale_loads[:7]:
-            load_w1_scales(w, r)
-        w1_words = [load_w1_words(0)]
-        load_w1_scales(*w1_scale_loads[7])
-        w1_words.append(load_w1_words(1))
+        for w in range(2):
+            for r in range(4):
+                load_w1_scales(w, r)
+        w1_words = [load_w1_words(w) for w in range(2)]
 
-        def look_up_scales(c):
-            picked = []
+        def look_up_scales():
+            picked = held("picked", [P, 2, J // 4], I32)
             for s in range(2):
-                tag = f"picked{s}" if c == 0 else f"both0{s}"
-                tile = held(f"picked{c}{s}", [P, CH // 4], I32, tag=tag)
-                nc.vector.tensor_copy(
-                    tile[:].bitcast(U8),
-                    tab_sc[:].bitcast(U8).indirect(lists[s][:, c * CH_COLS : (c + 1) * CH_COLS]),
-                )
-                picked.append(tile)
+                nc.vector.tensor_copy(picked[:, s, :].bitcast(U8), tab_sc[:].bitcast(U8).indirect(lists[s][:]))
             return picked
 
-        def move_scales(c, picked):
-            planes = []
-            for s in range(2):
-                down = moved[:, 2 * c + s, :]
-                nc.sync.dma_start(moved[0 : P - PASS_ROWS, 2 * c + s, :], picked[s][PASS_ROWS:P, :])
-                planes.append((picked[s][:], down))
-            return planes
+        def move_scales(picked):
+            for a in range(PASSES):
+                for r in range(4):
+                    first = SCALE_BASE + PASS_ROWS * a + r
+                    nc.sync.dma_start(planes[r:P:32, a, :, :], picked[first : first + 13 : 4, :, :])
 
         def look_up_words(c):
             both = []
@@ -140,7 +127,7 @@ def tile_list_msg_tanh_res_gate_kernel(
                 parted.append(apart)
             return parted
 
-        def first_layer(jt, parted, planes):
+        def first_layer(jt, parted, offset=None):
             cols = slice((jt % 4) * P, (jt % 4 + 1) * P)
             acc = psum.tile([P, R], F32, name=f"acc{jt}", tag=f"a{jt % 4}")
             for i in range(2 * PASSES):
@@ -148,30 +135,26 @@ def tile_list_msg_tanh_res_gate_kernel(
                 nc.tensor.matmul_mx(
                     out=acc[:],
                     lhsT=parted[s][:, a, cols].bitcast(FP4X4),
-                    lhsT_scale=planes[s][a].bitcast(U8)[:, cols],
+                    lhsT_scale=planes[:, a, s, :].bitcast(U8)[:, jt * P : (jt + 1) * P],
                     rhs=w1_words[s][:, a, :].bitcast(FP4X4),
                     rhs_scale=w1_sc[:, PASSES * s + a, :].bitcast(U8),
                     start=(i == 0),
                     stop=(i == 2 * PASSES - 1),
                 )
-            th = ring.tile([P, PACK, P], F32, name="th")
+            th = held(f"th{jt}", [P, PACK, P], F32, offset=offset)
             nc.scalar.activation(th[:], acc[:].rearrange("j (m t) -> j t m", t=PACK), TANH)
             return th
 
-        def turn(g, half, th, banks):
+        def hidden(g, ths, h_grouped, tags, h_rows):
+            banks = [psum.tile([P, 2, GROUP], F32, name=f"turned{g}{u}", tag=tags[u]) for u in range(2)]
             for t in range(PACK):
-                nc.tensor.transpose(banks[t // 2][:, t % 2, half * P : (half + 1) * P], th[:, t, :], ident[:])
-
-        def hidden(g, ths, h_grouped):
-            banks = [
-                psum.tile([P, 2, GROUP], F32, name=f"turned{g}{u}", tag=f"t{2 * (g % 2) + u}") for u in range(2)
-            ]
-            for half in range(2):
-                turn(g, half, ths[half], banks)
-            h_rows = held(f"h_rows{g}", [P, PACK, GROUP], BF16)
+                for half in range(2):
+                    nc.tensor.transpose(
+                        banks[t // 2][:, t % 2, half * P : (half + 1) * P], ths[half][:, t, :], ident[:]
+                    )
             for t in range(PACK):
                 nc.scalar.activation(h_rows[:, t, :], banks[t // 2][:, t % 2, :], COPY, scale=sm_sb[:, t : t + 1])
-            nc.scalar.copy(h_grouped, h_rows[:].rearrange("p t j -> p j t"))
+            nc.scalar.copy(h_grouped, h_rows.rearrange("p t j -> p j t"))
 
         def quantise(name, h_grouped, width, tag=None, offset=None):
             codes = held(f"h_codes{name}", [P, width], U32, tag=tag, offset=offset)
@@ -243,23 +226,29 @@ def tile_list_msg_tanh_res_gate_kernel(
             nc.gpsimd.memset(window[:], 0.0)
             windows.append(window)
 
-        picked_0 = look_up_scales(0)
-        planes_0 = move_scales(0, picked_0)
-        parted_0 = look_up_words(0)
-
-        sm_sb = held("sm_sb", [P, PACK], F32)
-        nc.sync.dma_start(sm_sb[:], sm.rearrange("(p t) -> p t", t=PACK))
+        picked = look_up_scales()
+        wgo_dealt = held("wgo_dealt", [P, J // P], F32)
+        nc.sync.dma_start(wgo_dealt[:], wgo[0].rearrange("(p c) -> p c", p=P))
         wgo_sb = held("wgo_sb", [P, J], F32)
-        nc.sync.dma_start(wgo_sb[:], wgo)
-        g_sb = {nt: load_gate_rows(nt) for nt in (0, 2)}
-        for q in range(QUADS):
-            load_wd_scales(0, q)
-
-        picked_1 = look_up_scales(1)
-        planes_1 = move_scales(1, picked_1)
+        for u in range(2):
+            spread = psum.tile([P, PACK, P], F32, name=f"spread{u}", tag=f"t{2 + u}")
+            for c in range(PACK):
+                column = wgo_dealt[:, PACK * u + c : PACK * u + c + 1]
+                nc.tensor.transpose(spread[:, c, :], column.to_broadcast([P, P]), ident[:])
+            nc.scalar.copy(
+                wgo_sb[:].rearrange("m (p u c) -> m p u c", u=2, c=PACK)[:, :, u, :],
+                spread[:].rearrange("m c p -> m p c"),
+            )
+        move_scales(picked)
+        parted_0 = look_up_words(0)
         parted_1 = look_up_words(1)
 
-        for nt in (1, 3):
+        g_sb = {0: load_gate_rows(0)}
+        sm_sb = held("sm_sb", [P, PACK], F32)
+        nc.sync.dma_start(sm_sb[:], sm.rearrange("(p t) -> p t", t=PACK))
+        for q in range(QUADS):
+            load_wd_scales(0, q)
+        for nt in range(1, N_TILES):
             g_sb[nt] = load_gate_rows(nt)
         for q in range(QUADS):
             load_wd_scales(1, q)
@@ -270,34 +259,35 @@ def tile_list_msg_tanh_res_gate_kernel(
 
         grouped = [held(f"h_grouped{c}", [P, CH, PACK], BF16) for c in range(CHUNKS)]
         halves = (slice(0, GROUP), slice(GROUP, CH))
-        ths = [first_layer(jt, parted_0, planes_0) for jt in range(4)]
-        for g in range(2):
-            hidden(g, ths[2 * g : 2 * g + 2], grouped[0][:, halves[g], :])
-        ths_late = [first_layer(jt, parted_1, planes_1) for jt in range(4, 8)]
+        ths = [first_layer(jt, parted_0) for jt in range(4)]
+        rows_0 = held("h_rows0", [P, PACK, GROUP], BF16)
+        hidden(0, ths[0:2], grouped[0][:, halves[0], :], ("t0", "t1"), rows_0[:])
+        rows_1 = held("h_rows1", [P, 6 * PACK, GROUP], BF16, offset=0)
+        hidden(1, ths[2:4], grouped[0][:, halves[1], :], ("t2", "t3"), rows_1[:, 0:PACK, :])
+        ths_late = [first_layer(jt, parted_1, offset=(jt - 4) * 4 * R) for jt in range(4, 8)]
         gates = {}
         gate(0, 0, J)
         new_window("g0")
-        gate(2, 0, CH)
         gate(1, 0, J)
-        h_0 = quantise("0", grouped[0], CH, offset=0)
+        gate(2, 0, J)
+        h_0 = quantise("0", grouped[0], CH, tag="g2")
         new_window("h_grouped0")
-        gate(2, CH, CH, offset=4 * CH)
-        new_window("g2")
-        gate(3, 0, J)
+        gate(3, 0, J, offset=4 * 4 * R)
+        new_window("g3")
         early = [held(f"y_early{nt}", [P, CH], F32) for nt in range(2)]
-        for nt, tag in enumerate(("t0", "t2")):
+        for nt, tag in enumerate(("t0", "t1")):
             message(nt, h_0, bank(tag), early[nt][:])
         for g in range(2):
-            hidden(2 + g, ths_late[2 * g : 2 * g + 2], grouped[1][:, halves[g], :])
+            rows = held(f"h_rows{2 + g}", [P, PACK, GROUP], BF16)
+            hidden(2 + g, ths_late[2 * g : 2 * g + 2], grouped[1][:, halves[g], :], ("t0", "t1"), rows[:])
         for nt in range(2):
             scatter(nt, 0, early[nt][:], gates[nt, 0][:, 0:CH])
         h_1 = quantise("1", grouped[1], CH, "y_early0")
         y_2 = held("y_2", [P, CH], F32, tag="h_rows3")
-        scatter(2, 0, message(2, h_0, bank("a0"), y_2[:]), gates[2, 0][:])
-        late_gates = (gates[0, 0][:, CH:J], gates[1, 0][:, CH:J], gates[2, CH][:])
-        for nt in range(WINDOWS):
-            scatter(nt, CH, message(nt, h_1, bank(f"a{nt + 1}"), staging()), late_gates[nt])
+        scatter(2, 0, message(2, h_0, bank("t2"), y_2[:]), gates[2, 0][:, 0:CH])
+        for nt, tag in enumerate(("a0", "a1", "a2")):
+            scatter(nt, CH, message(nt, h_1, bank(tag), staging()), gates[nt, 0][:, CH:J])
         y_last = held("y_last", [P, J], F32)
         for c, h in enumerate((h_0, h_1)):
-            message(3, h, bank(f"t{c}"), y_last[:, c * CH : (c + 1) * CH])
+            message(3, h, bank(("a3", "t3")[c]), y_last[:, c * CH : (c + 1) * CH])
         scatter(3, 0, y_last[:], gates[3, 0][:])

@@ -60,11 +60,10 @@ def tile_list_msg_tanh_res_gate_kernel(
         windows = []
         nc.vector.memset(w1_sc[:], 0)
         nc.vector.memset(tab_sc[0:SCALE_BASE, :], 0)
+        nc.vector.memset(planes[:], 0)
 
         ident = held("ident", [P, P], F32)
         make_identity(nc, ident[:])
-        nc.gpsimd.memset(planes[:], 0)
-        nc.gpsimd.memset(wd_sc[:], 0)
 
         nc.sync.dma_start(src_list[:], offs)
         nc.sync.dma_start(tab_sc[SCALE_BASE:P, :], tab_scales.rearrange("a q t -> (a q) t").bitcast(I32))
@@ -74,7 +73,7 @@ def tile_list_msg_tanh_res_gate_kernel(
 
         def load_w1_scales(w, r):
             scales = (ws_scales, wt_scales)[w]
-            nc.sync.dma_start(
+            (nc.sync, nc.gpsimd)[w].dma_start(
                 w1_sc[r:P:32, PASSES * w : PASSES * (w + 1), :],
                 scales.rearrange("a (q r) n -> r q a n", r=4)[r].bitcast(I32),
             )
@@ -96,6 +95,20 @@ def tile_list_msg_tanh_res_gate_kernel(
         for w in range(2):
             for r in range(4):
                 load_w1_scales(w, r)
+        nc.gpsimd.memset(wd_sc[:], 0)
+        g_sb = {0: load_gate_rows(0)}
+        wgo_dealt = held("wgo_dealt", [P, J // P], F32)
+        nc.sync.dma_start(wgo_dealt[:], wgo[0].rearrange("(p c) -> p c", p=P))
+        wgo_sb = held("wgo_sb", [P, J], F32)
+        for u in range(2):
+            spread = psum.tile([P, PACK, P], F32, name=f"spread{u}", tag=f"t{2 + u}")
+            for c in range(PACK):
+                column = wgo_dealt[:, PACK * u + c : PACK * u + c + 1]
+                nc.tensor.transpose(spread[:, c, :], column.to_broadcast([P, P]), ident[:])
+            nc.scalar.copy(
+                wgo_sb[:].rearrange("m (p u c) -> m p u c", u=2, c=PACK)[:, :, u, :],
+                spread[:].rearrange("m c p -> m p c"),
+            )
         w1_words = [load_w1_words(w) for w in range(2)]
 
         def look_up_scales():
@@ -145,16 +158,21 @@ def tile_list_msg_tanh_res_gate_kernel(
             nc.scalar.activation(th[:], acc[:].rearrange("j (m t) -> j t m", t=PACK), TANH)
             return th
 
-        def hidden(g, ths, h_grouped, tags, h_rows):
-            banks = [psum.tile([P, 2, GROUP], F32, name=f"turned{g}{u}", tag=tags[u]) for u in range(2)]
+        def hidden(name, ths, h_grouped, tags, h_rows):
+            per_bank = PACK // len(ths)
+            banks = [psum.tile([P, per_bank, len(ths) * P], F32, name=f"turned{name}{tag}", tag=tag) for tag in tags]
             for t in range(PACK):
-                for half in range(2):
+                for i, th in enumerate(ths):
                     nc.tensor.transpose(
-                        banks[t // 2][:, t % 2, half * P : (half + 1) * P], ths[half][:, t, :], ident[:]
+                        banks[t // per_bank][:, t % per_bank, i * P : (i + 1) * P], th[:, t, :], ident[:]
                     )
             for t in range(PACK):
-                nc.scalar.activation(h_rows[:, t, :], banks[t // 2][:, t % 2, :], COPY, scale=sm_sb[:, t : t + 1])
-            nc.scalar.copy(h_grouped, h_rows.rearrange("p t j -> p j t"))
+                nc.scalar.activation(
+                    h_rows[:, t, :], banks[t // per_bank][:, t % per_bank, :], COPY, scale=sm_sb[:, t : t + 1]
+                )
+            nc.scalar.copy(
+                h_grouped.rearrange("p (c i) t -> p c t i", i=4), h_rows.rearrange("p t (c i) -> p c t i", i=4)
+            )
 
         def quantise(name, h_grouped, width, tag=None, offset=None):
             codes = held(f"h_codes{name}", [P, width], U32, tag=tag, offset=offset)
@@ -227,43 +245,46 @@ def tile_list_msg_tanh_res_gate_kernel(
             windows.append(window)
 
         picked = look_up_scales()
-        wgo_dealt = held("wgo_dealt", [P, J // P], F32)
-        nc.sync.dma_start(wgo_dealt[:], wgo[0].rearrange("(p c) -> p c", p=P))
-        wgo_sb = held("wgo_sb", [P, J], F32)
-        for u in range(2):
-            spread = psum.tile([P, PACK, P], F32, name=f"spread{u}", tag=f"t{2 + u}")
-            for c in range(PACK):
-                column = wgo_dealt[:, PACK * u + c : PACK * u + c + 1]
-                nc.tensor.transpose(spread[:, c, :], column.to_broadcast([P, P]), ident[:])
-            nc.scalar.copy(
-                wgo_sb[:].rearrange("m (p u c) -> m p u c", u=2, c=PACK)[:, :, u, :],
-                spread[:].rearrange("m c p -> m p c"),
-            )
         move_scales(picked)
         parted_0 = look_up_words(0)
         parted_1 = look_up_words(1)
 
-        g_sb = {0: load_gate_rows(0)}
         sm_sb = held("sm_sb", [P, PACK], F32)
         nc.sync.dma_start(sm_sb[:], sm.rearrange("(p t) -> p t", t=PACK))
-        for q in range(QUADS):
-            load_wd_scales(0, q)
-        for nt in range(1, N_TILES):
+        for nt in (1, 2):
             g_sb[nt] = load_gate_rows(nt)
         for q in range(QUADS):
-            load_wd_scales(1, q)
+            load_wd_scales(0, q)
         wd8 = held("wd8", [P, N], I32)
         nc.sync.dma_start(wd8[:], wd8_words[0].rearrange("p n i -> p (n i)").bitcast(I32))
         wd4 = held("wd4", [P, N // 2], I32)
         nc.sync.dma_start(wd4[:], wd4_words[0].bitcast(I32))
+        g_sb[3] = load_gate_rows(3)
+        for q in range(QUADS):
+            load_wd_scales(1, q)
+
+        warm = psum.tile([P, R], F32, name="warm", tag="a3")
+        for i in range(3):
+            nc.tensor.matmul_mx(
+                out=warm[:],
+                lhsT=w1_words[0][:, 0, 0 : P // 2].bitcast(FP4X4),
+                lhsT_scale=w1_sc[:, 0, :].bitcast(U8)[:, 0:P],
+                rhs=w1_words[0][:, 1, :].bitcast(FP4X4),
+                rhs_scale=w1_sc[:, 1, :].bitcast(U8),
+                start=(i == 0),
+                stop=(i == 2),
+            )
 
         grouped = [held(f"h_grouped{c}", [P, CH, PACK], BF16) for c in range(CHUNKS)]
         halves = (slice(0, GROUP), slice(GROUP, CH))
-        ths = [first_layer(jt, parted_0) for jt in range(4)]
-        rows_0 = held("h_rows0", [P, PACK, GROUP], BF16)
-        hidden(0, ths[0:2], grouped[0][:, halves[0], :], ("t0", "t1"), rows_0[:])
-        rows_1 = held("h_rows1", [P, 6 * PACK, GROUP], BF16, offset=0)
-        hidden(1, ths[2:4], grouped[0][:, halves[1], :], ("t2", "t3"), rows_1[:, 0:PACK, :])
+        ths = [first_layer(0, parted_0)]
+        for jt in range(4):
+            if jt < 3:
+                ths.append(first_layer(jt + 1, parted_0))
+                rows = held(f"h_early{jt}", [P, PACK, P], BF16)
+            else:
+                rows = held(f"h_early{jt}", [P, 12 * PACK, P], BF16, offset=0)
+            hidden(f"early{jt}", [ths[jt]], grouped[0][:, jt * P : (jt + 1) * P, :], (f"t{jt}",), rows[:, 0:PACK, :])
         ths_late = [first_layer(jt, parted_1, offset=(jt - 4) * 4 * R) for jt in range(4, 8)]
         gates = {}
         gate(0, 0, J)

@@ -66,7 +66,7 @@ def tile_list_msg_tanh_res_gate_kernel(
         make_identity(nc, ident[:])
 
         nc.sync.dma_start(src_list[:], offs)
-        nc.sync.dma_start(tab_sc[SCALE_BASE:P, :], tab_scales.rearrange("a q t -> (a q) t").bitcast(I32))
+        nc.scalar.dma_start(tab_sc[SCALE_BASE:P, :], tab_scales.rearrange("a q t -> (a q) t").bitcast(I32))
         nc.sync.dma_start(dst_list[:], offs2)
         table = held("table", [P, T], I32)
         nc.sync.dma_start(table[:], tab_words[0].rearrange("p t b -> p (t b)").bitcast(I32))
@@ -144,7 +144,7 @@ def tile_list_msg_tanh_res_gate_kernel(
             cols = slice((jt % 4) * P, (jt % 4 + 1) * P)
             acc = psum.tile([P, R], F32, name=f"acc{jt}", tag=f"a{jt % 4}")
             for i in range(2 * PASSES):
-                a, s = divmod(i if jt == 0 else 2 * PASSES - 1 - i, 2)
+                s, a = divmod(i if jt == 0 else 2 * PASSES - 1 - i, PASSES)
                 nc.tensor.matmul_mx(
                     out=acc[:],
                     lhsT=parted[s][:, a, cols].bitcast(FP4X4),
@@ -291,7 +291,7 @@ def tile_list_msg_tanh_res_gate_kernel(
         new_window("g0")
         gate(1, 0, J)
         gate(2, 0, J)
-        h_0 = quantise("0", grouped[0], CH, tag="g2")
+        h_0 = quantise("0", grouped[0], CH)
         new_window("h_grouped0")
         gate(3, 0, J, offset=4 * 4 * R)
         new_window("g3")
@@ -305,10 +305,10 @@ def tile_list_msg_tanh_res_gate_kernel(
             scatter(nt, 0, early[nt][:], gates[nt, 0][:, 0:CH])
         h_1 = quantise("1", grouped[1], CH, "y_early0")
         y_2 = held("y_2", [P, CH], F32, tag="h_rows3")
-        scatter(2, 0, message(2, h_0, bank("t2"), y_2[:]), gates[2, 0][:, 0:CH])
+        scatter(2, 0, message(2, h_0, bank("t0"), y_2[:]), gates[2, 0][:, 0:CH])
         for nt, tag in enumerate(("a0", "a1", "a2")):
             scatter(nt, CH, message(nt, h_1, bank(tag), staging()), gates[nt, 0][:, CH:J])
-        y_last = held("y_last", [P, J], F32)
+        y_last = held("y_last", [P, J], F32, tag="h_grouped1")
         for c, h in enumerate((h_0, h_1)):
-            message(3, h, bank(("a3", "t3")[c]), y_last[:, c * CH : (c + 1) * CH])
+            message(3, h, bank(("t1", "t3")[c]), y_last[:, c * CH : (c + 1) * CH])
         scatter(3, 0, y_last[:], gates[3, 0][:])

@@ -30,7 +30,7 @@ N_TILES = N // P
 GROUP = 256
 PASS_ROWS = 16
 SCALE_BASE = 96
-WINDOWS = 3
+SHORT = 3 * P
 
 
 def tile_list_msg_tanh_res_gate_kernel(
@@ -40,13 +40,9 @@ def tile_list_msg_tanh_res_gate_kernel(
     nc = tc.nc
     with ExitStack() as ctx:
         keep = ctx.enter_context(tc.tile_pool(name="keep", bufs=1))
-        msgs = ctx.enter_context(tc.tile_pool(name="msgs", bufs=3))
-        shared = ctx.enter_context(tc.tile_pool(name="shared", bufs=1))
         psum = ctx.enter_context(tc.psum_pool(name="psum", bufs=1))
 
-        def held(name, shape, dtype, tag=None, offset=None):
-            if offset is not None:
-                return shared.tile(shape, dtype, name=name, align_bytes=64, offset=offset)
+        def held(name, shape, dtype, tag=None):
             return keep.tile(shape, dtype, name=name, tag=tag or name, align_bytes=64)
 
         src_list = keep.tile([P, LIST_COLS], U16, name="src_list")
@@ -54,13 +50,14 @@ def tile_list_msg_tanh_res_gate_kernel(
         lists = (src_list, dst_list)
 
         tab_sc = held("tab_sc", [P, T // 4], I32)
-        w1_sc = held("w1_sc", [P, 2 * PASSES, R // 4], I32)
+        w1_sc = [held(f"w1_sc{w}", [P, PASSES, R // 4], I32) for w in range(2)]
         planes = held("planes", [P, PASSES, 2, J // 4], I32)
         wd_sc = held("wd_sc", [P, 2, N // 4], I32)
         windows = []
-        nc.vector.memset(w1_sc[:], 0)
+        nc.vector.memset(w1_sc[0][:], 0)
         nc.vector.memset(tab_sc[0:SCALE_BASE, :], 0)
         nc.vector.memset(planes[:], 0)
+        nc.vector.memset(w1_sc[1][:], 0)
 
         ident = held("ident", [P, P], F32)
         make_identity(nc, ident[:])
@@ -74,7 +71,7 @@ def tile_list_msg_tanh_res_gate_kernel(
         def load_w1_scales(w, r):
             scales = (ws_scales, wt_scales)[w]
             (nc.sync, nc.gpsimd)[w].dma_start(
-                w1_sc[r:P:32, PASSES * w : PASSES * (w + 1), :],
+                w1_sc[w][r:P:32, :, :],
                 scales.rearrange("a (q r) n -> r q a n", r=4)[r].bitcast(I32),
             )
 
@@ -88,7 +85,7 @@ def tile_list_msg_tanh_res_gate_kernel(
             nc.sync.dma_start(wd_sc[32 * q : 32 * q + 4, w, :], scales[0, 4 * q : 4 * q + 4, :].bitcast(I32))
 
         def load_gate_rows(nt):
-            rows = held(f"g{nt}", [P, T], F32, offset=None)
+            rows = held(f"g{nt}", [P, T], F32)
             nc.sync.dma_start(rows[:], gT[nt * P : (nt + 1) * P, :])
             return rows
 
@@ -140,9 +137,9 @@ def tile_list_msg_tanh_res_gate_kernel(
                 parted.append(apart)
             return parted
 
-        def first_layer(jt, parted, offset=None):
+        def first_layer(jt, parted, tag):
             cols = slice((jt % 4) * P, (jt % 4 + 1) * P)
-            acc = psum.tile([P, R], F32, name=f"acc{jt}", tag=f"a{jt % 4}")
+            acc = psum.tile([P, R], F32, name=f"acc{jt}", tag=tag)
             for i in range(2 * PASSES):
                 s, a = divmod(i if jt == 0 else 2 * PASSES - 1 - i, PASSES)
                 nc.tensor.matmul_mx(
@@ -150,11 +147,11 @@ def tile_list_msg_tanh_res_gate_kernel(
                     lhsT=parted[s][:, a, cols].bitcast(FP4X4),
                     lhsT_scale=planes[:, a, s, :].bitcast(U8)[:, jt * P : (jt + 1) * P],
                     rhs=w1_words[s][:, a, :].bitcast(FP4X4),
-                    rhs_scale=w1_sc[:, PASSES * s + a, :].bitcast(U8),
+                    rhs_scale=w1_sc[s][:, a, :].bitcast(U8),
                     start=(i == 0),
                     stop=(i == 2 * PASSES - 1),
                 )
-            th = held(f"th{jt}", [P, PACK, P], F32, offset=offset)
+            th = held(f"th{jt}", [P, PACK, P], F32)
             nc.scalar.activation(th[:], acc[:].rearrange("j (m t) -> j t m", t=PACK), TANH)
             return th
 
@@ -174,70 +171,53 @@ def tile_list_msg_tanh_res_gate_kernel(
                 h_grouped.rearrange("p (c i) t -> p c t i", i=4), h_rows.rearrange("p t (c i) -> p c t i", i=4)
             )
 
-        def quantise(name, h_grouped, width, tag=None, offset=None):
-            codes = held(f"h_codes{name}", [P, width], U32, tag=tag, offset=offset)
-            scales = held(f"h_sc{name}", [P, width], U8)
+        def quantise(c, cols):
             nc.vector.quantize_mx(
-                out=codes[:].bitcast(FP8X4),
-                scales=scales[:],
-                in_=h_grouped[:].rearrange("p j t -> p (j t)"),
+                out=codes[c][:, cols].bitcast(FP8X4),
+                scales=h_sc[c][:, cols],
+                in_=grouped[c][:, cols, :].rearrange("p j t -> p (j t)"),
             )
-            return codes, scales
 
-        def gate(nt, first, count, offset=None):
-            tile = held(f"gate{nt}_{first}", [P, count], F32, offset=offset)
-            nc.vector.tensor_tensor(
-                tile[:],
-                g_sb[nt][:].indirect(src_list[:, first // 16 : (first + count) // 16]),
-                wgo_sb[:, first : first + count],
-                MULT,
-            )
-            gates[nt, first] = tile
+        def gate(nt, tag=None):
+            tile = held(f"gate{nt}", [P, J], F32, tag=tag)
+            nc.vector.tensor_tensor(tile[:], g_sb[nt][:].indirect(src_list[:]), wgo_sb[:], MULT)
+            return tile
 
-        def second_layer(nt, h, cols, y):
+        def second_layer(nt, c, cols, y):
             rows = slice(nt * P, (nt + 1) * P)
-            codes, scales = h
-            nc.tensor.matmul_mx(
-                out=y,
-                lhsT=wd4[:, nt * P // 2 : (nt + 1) * P // 2].bitcast(FP4X4),
-                lhsT_scale=wd_sc[:, 0, :].bitcast(U8)[:, rows],
-                rhs=codes[:, cols].bitcast(FP8X4),
-                rhs_scale=scales[:, cols],
-                start=True,
-                stop=False,
-            )
-            nc.tensor.matmul_mx(
-                out=y,
-                lhsT=wd8[:, rows].bitcast(FP8X4),
-                lhsT_scale=wd_sc[:, 1, :].bitcast(U8)[:, rows],
-                rhs=codes[:, cols].bitcast(FP8X4),
-                rhs_scale=scales[:, cols],
-                start=False,
-                stop=True,
-            )
+            weights = (wd4[:, nt * P // 2 : (nt + 1) * P // 2].bitcast(FP4X4), wd8[:, rows].bitcast(FP8X4))
+            for w in range(2):
+                nc.tensor.matmul_mx(
+                    out=y,
+                    lhsT=weights[w],
+                    lhsT_scale=wd_sc[:, w, :].bitcast(U8)[:, rows],
+                    rhs=codes[c][:, cols].bitcast(FP8X4),
+                    rhs_scale=h_sc[c][:, cols],
+                    start=(w == 0),
+                    stop=(w == 1),
+                )
 
-        def message(nt, h, y, y_sb):
-            second_layer(nt, h, slice(0, CH), y[:])
+        def message(nt, c, tag, y_sb):
+            y = psum.tile([P, CH], F32, name=f"y{nt}{c}", tag=tag)
+            second_layer(nt, c, slice(0, CH), y[:])
             nc.scalar.copy(y_sb, y[:])
-            return y_sb
 
-        def scatter(nt, first, y_sb, gate_values):
+        def short_message(nt, tag, cols):
+            y = psum.tile([P, cols.stop - cols.start], F32, name=f"y_short{nt}{tag}", tag=tag)
+            for first in range(cols.start, cols.stop, P):
+                second_layer(nt, 0, slice(first, first + P), y[:, first - cols.start : first - cols.start + P])
+            nc.scalar.copy(early[nt][:, cols], y[:])
+
+        def scatter(nt, first, y_sb):
             count = y_sb.shape[1]
-            window = windows[nt % WINDOWS]
             nc.vector.tensor_tensor(
-                window[:].indirect(dst_list[:, first // 16 : (first + count) // 16]),
+                windows[nt][:].indirect(dst_list[:, first // 16 : (first + count) // 16]),
                 y_sb,
-                gate_values,
+                gates[nt][:, first : first + count],
                 MULT,
             )
             if first + count == J:
-                nc.sync.dma_start(out[nt * P : (nt + 1) * P, :], window[:])
-
-        def bank(tag):
-            return psum.tile([P, CH], F32, name=f"y_{tag}", tag=tag)
-
-        def staging():
-            return msgs.tile([P, CH], F32, name="y_sb")[:]
+                nc.sync.dma_start(out[nt * P : (nt + 1) * P, :], windows[nt][:])
 
         def new_window(tag):
             window = held(f"window{len(windows)}", [P, T], F32, tag=tag)
@@ -251,7 +231,7 @@ def tile_list_msg_tanh_res_gate_kernel(
 
         sm_sb = held("sm_sb", [P, PACK], F32)
         nc.sync.dma_start(sm_sb[:], sm.rearrange("(p t) -> p t", t=PACK))
-        for nt in (1, 2):
+        for nt in range(1, N_TILES):
             g_sb[nt] = load_gate_rows(nt)
         for q in range(QUADS):
             load_wd_scales(0, q)
@@ -259,56 +239,59 @@ def tile_list_msg_tanh_res_gate_kernel(
         nc.sync.dma_start(wd8[:], wd8_words[0].rearrange("p n i -> p (n i)").bitcast(I32))
         wd4 = held("wd4", [P, N // 2], I32)
         nc.sync.dma_start(wd4[:], wd4_words[0].bitcast(I32))
-        g_sb[3] = load_gate_rows(3)
         for q in range(QUADS):
             load_wd_scales(1, q)
 
-        warm = psum.tile([P, R], F32, name="warm", tag="a3")
-        for i in range(3):
-            nc.tensor.matmul_mx(
-                out=warm[:],
-                lhsT=w1_words[0][:, 0, 0 : P // 2].bitcast(FP4X4),
-                lhsT_scale=w1_sc[:, 0, :].bitcast(U8)[:, 0:P],
-                rhs=w1_words[0][:, 1, :].bitcast(FP4X4),
-                rhs_scale=w1_sc[:, 1, :].bitcast(U8),
-                start=(i == 0),
-                stop=(i == 2),
-            )
-
         grouped = [held(f"h_grouped{c}", [P, CH, PACK], BF16) for c in range(CHUNKS)]
-        halves = (slice(0, GROUP), slice(GROUP, CH))
-        ths = [first_layer(0, parted_0)]
+        codes = [held(f"h_codes{c}", [P, CH], U32) for c in range(CHUNKS)]
+        h_sc = [held(f"h_sc{c}", [P, CH], U8) for c in range(CHUNKS)]
+        ths = [first_layer(0, parted_0, "a0")]
         for jt in range(4):
-            if jt < 3:
-                ths.append(first_layer(jt + 1, parted_0))
-                rows = held(f"h_early{jt}", [P, PACK, P], BF16)
-            else:
-                rows = held(f"h_early{jt}", [P, 12 * PACK, P], BF16, offset=0)
-            hidden(f"early{jt}", [ths[jt]], grouped[0][:, jt * P : (jt + 1) * P, :], (f"t{jt}",), rows[:, 0:PACK, :])
-        ths_late = [first_layer(jt, parted_1, offset=(jt - 4) * 4 * R) for jt in range(4, 8)]
-        gates = {}
-        gate(0, 0, J)
+            if jt < 2:
+                ths.append(first_layer(jt + 1, parted_0, f"a{jt + 1}"))
+            if jt == 3:
+                ths.append(first_layer(jt, parted_0, f"a{jt}"))
+            rows = held(f"h_early{jt}", [P, PACK, P], BF16)
+            hidden(f"early{jt}", [ths[jt]], grouped[0][:, jt * P : (jt + 1) * P, :], (f"t{jt}",), rows[:])
+        ths_late = [first_layer(jt, parted_1, f"a{jt - 4}") for jt in range(4, 7)]
+        new_window("both11")
+        gates = [gate(0)]
         new_window("g0")
-        gate(1, 0, J)
-        gate(2, 0, J)
-        h_0 = quantise("0", grouped[0], CH)
+        gates.extend([gate(1), gate(2)])
+        quantise(0, slice(0, GROUP))
+        quantise(0, slice(GROUP, SHORT))
+        gates.append(gate(3, tag="h_early2"))
+        quantise(0, slice(SHORT, CH))
         new_window("h_grouped0")
-        gate(3, 0, J, offset=4 * 4 * R)
-        new_window("g3")
-        early = [held(f"y_early{nt}", [P, CH], F32) for nt in range(2)]
-        for nt, tag in enumerate(("t0", "t1")):
-            message(nt, h_0, bank(tag), early[nt][:])
-        for g in range(2):
-            rows = held(f"h_rows{2 + g}", [P, PACK, GROUP], BF16)
-            hidden(2 + g, ths_late[2 * g : 2 * g + 2], grouped[1][:, halves[g], :], ("t0", "t1"), rows[:])
+        early = [held(f"y_early{nt}", [P, SHORT], F32) for nt in range(2)]
+        short_message(0, "t0", slice(0, GROUP))
+        short_message(0, "t2", slice(GROUP, SHORT))
+        short_message(1, "t1", slice(0, SHORT))
+        rows = held("h_rows2", [P, PACK, GROUP], BF16)
+        hidden(2, ths_late[0:2], grouped[1][:, 0:GROUP, :], ("t0", "t2"), rows[:])
+        ths_late.append(first_layer(7, parted_1, "t1"))
+        y_2 = held("y_2", [P, CH], F32)
+        message(2, 0, "t0", y_2[:])
+        rows = held("h_rows3", [P, PACK, GROUP], BF16)
+        hidden(3, ths_late[2:4], grouped[1][:, GROUP:CH, :], ("t2", "t1"), rows[:])
         for nt in range(2):
-            scatter(nt, 0, early[nt][:], gates[nt, 0][:, 0:CH])
-        h_1 = quantise("1", grouped[1], CH, "y_early0")
-        y_2 = held("y_2", [P, CH], F32, tag="h_rows3")
-        scatter(2, 0, message(2, h_0, bank("t0"), y_2[:]), gates[2, 0][:, 0:CH])
-        for nt, tag in enumerate(("a0", "a1", "a2")):
-            scatter(nt, CH, message(nt, h_1, bank(tag), staging()), gates[nt, 0][:, CH:J])
-        y_last = held("y_last", [P, J], F32, tag="h_grouped1")
-        for c, h in enumerate((h_0, h_1)):
-            message(3, h, bank(("t1", "t3")[c]), y_last[:, c * CH : (c + 1) * CH])
-        scatter(3, 0, y_last[:], gates[3, 0][:])
+            scatter(nt, 0, early[nt][:])
+        new_window("y_early0")
+        scatter(2, 0, y_2[:])
+        quantise(1, slice(0, CH))
+        rest = J - SHORT
+        late = held("y_late", [P, CH + 2 * rest], F32, tag="h_rows3")
+        message(3, 0, "t2", late[:, 0:CH])
+        scatter(3, 0, late[:, 0:CH])
+        long_rows = late[:, CH:].rearrange("p (n j) -> p n j", n=2)
+        fourth = psum.tile([P, 2, P], F32, name="y_fourth", tag="t1")
+        for nt in range(2):
+            second_layer(nt, 0, slice(SHORT, CH), fourth[:, nt, :])
+        nc.scalar.copy(long_rows[:, :, 0:P], fourth[:])
+        for nt in range(2, N_TILES):
+            y_sb = held(f"y_end{nt}", [P, CH], F32)
+            message(nt, 1, f"a{nt}", y_sb[:])
+            scatter(nt, CH, y_sb[:])
+        for nt in range(2):
+            message(nt, 1, f"a{nt}", long_rows[:, nt, P:])
+            scatter(nt, SHORT, long_rows[:, nt, :])

@@ -54,6 +54,12 @@ def tile_list_msg_tanh_res_gate_kernel(
         planes = held("planes", [P, PASSES, 2, J // 4], I32)
         wd_sc = held("wd_sc", [P, 2, N // 4], I32)
         windows = []
+
+        def new_window(tag):
+            window = held(f"window{len(windows)}", [P, T], F32, tag=tag)
+            nc.gpsimd.memset(window[:], 0.0)
+            windows.append(window)
+
         nc.vector.memset(w1_sc[0][:], 0)
         nc.vector.memset(tab_sc[0:SCALE_BASE, :], 0)
         nc.vector.memset(planes[:], 0)
@@ -93,6 +99,8 @@ def tile_list_msg_tanh_res_gate_kernel(
             for r in range(4):
                 load_w1_scales(w, r)
         nc.gpsimd.memset(wd_sc[:], 0)
+        new_window("window0")
+        new_window("window1")
         g_sb = {0: load_gate_rows(0)}
         wgo_dealt = held("wgo_dealt", [P, J // P], F32)
         nc.sync.dma_start(wgo_dealt[:], wgo[0].rearrange("(p c) -> p c", p=P))
@@ -219,11 +227,6 @@ def tile_list_msg_tanh_res_gate_kernel(
             if first + count == J:
                 nc.sync.dma_start(out[nt * P : (nt + 1) * P, :], windows[nt][:])
 
-        def new_window(tag):
-            window = held(f"window{len(windows)}", [P, T], F32, tag=tag)
-            nc.gpsimd.memset(window[:], 0.0)
-            windows.append(window)
-
         picked = look_up_scales()
         move_scales(picked)
         parted_0 = look_up_words(0)
@@ -262,7 +265,6 @@ def tile_list_msg_tanh_res_gate_kernel(
         quantise(0, slice(GROUP, SHORT))
         gates.append(gate(3, tag="h_early2"))
         quantise(0, slice(SHORT, CH))
-        new_window("h_grouped0")
         early = [held(f"y_early{nt}", [P, SHORT], F32) for nt in range(2)]
         short_message(0, "t0", slice(0, GROUP))
         short_message(0, "t2", slice(GROUP, SHORT))
@@ -276,7 +278,6 @@ def tile_list_msg_tanh_res_gate_kernel(
         hidden(3, ths_late[2:4], grouped[1][:, GROUP:CH, :], ("t2", "t1"), rows[:])
         for nt in range(2):
             scatter(nt, 0, early[nt][:])
-        new_window("y_early0")
         scatter(2, 0, y_2[:])
         quantise(1, slice(0, CH))
         rest = J - SHORT

@@ -100,7 +100,6 @@ def tile_list_msg_tanh_res_gate_kernel(
                 load_w1_scales(w, r)
         nc.gpsimd.memset(wd_sc[:], 0)
         new_window("window0")
-        new_window("window1")
         g_sb = {0: load_gate_rows(0)}
         wgo_dealt = held("wgo_dealt", [P, J // P], F32)
         nc.sync.dma_start(wgo_dealt[:], wgo[0].rearrange("(p c) -> p c", p=P))
@@ -265,6 +264,7 @@ def tile_list_msg_tanh_res_gate_kernel(
         quantise(0, slice(GROUP, SHORT))
         gates.append(gate(3, tag="h_early2"))
         quantise(0, slice(SHORT, CH))
+        new_window("h_grouped0")
         early = [held(f"y_early{nt}", [P, SHORT], F32) for nt in range(2)]
         short_message(0, "t0", slice(0, GROUP))
         short_message(0, "t2", slice(GROUP, SHORT))

@@ -76,7 +76,7 @@ def tile_list_msg_tanh_res_gate_kernel(
 
         def load_w1_scales(w, r):
             scales = (ws_scales, wt_scales)[w]
-            (nc.sync, nc.gpsimd)[w].dma_start(
+            (nc.gpsimd if w == 1 and r >= 2 else nc.sync).dma_start(
                 w1_sc[w][r:P:32, :, :],
                 scales.rearrange("a (q r) n -> r q a n", r=4)[r].bitcast(I32),
             )

@@ -260,8 +260,7 @@ def tile_list_msg_tanh_res_gate_kernel(
         gates = [gate(0)]
         new_window("g0")
         gates.extend([gate(1), gate(2)])
-        quantise(0, slice(0, GROUP))
-        quantise(0, slice(GROUP, SHORT))
+        quantise(0, slice(0, SHORT))
         gates.append(gate(3, tag="h_early2"))
         quantise(0, slice(SHORT, CH))
         new_window("h_grouped0")

@@ -76,7 +76,7 @@ def tile_list_msg_tanh_res_gate_kernel(
 
         def load_w1_scales(w, r):
             scales = (ws_scales, wt_scales)[w]
-            (nc.gpsimd if w == 1 and r >= 2 else nc.sync).dma_start(
+            nc.sync.dma_start(
                 w1_sc[w][r:P:32, :, :],
                 scales.rearrange("a (q r) n -> r q a n", r=4)[r].bitcast(I32),
             )
@@ -95,12 +95,15 @@ def tile_list_msg_tanh_res_gate_kernel(
             nc.sync.dma_start(rows[:], gT[nt * P : (nt + 1) * P, :])
             return rows
 
-        for w in range(2):
-            for r in range(4):
-                load_w1_scales(w, r)
+        for r in range(4):
+            load_w1_scales(0, r)
+        for r in range(2):
+            load_w1_scales(1, r)
         nc.gpsimd.memset(wd_sc[:], 0)
         new_window("window0")
         g_sb = {0: load_gate_rows(0)}
+        for r in range(2, 4):
+            load_w1_scales(1, r)
         wgo_dealt = held("wgo_dealt", [P, J // P], F32)
         nc.sync.dma_start(wgo_dealt[:], wgo[0].rearrange("(p c) -> p c", p=P))
         wgo_sb = held("wgo_sb", [P, J], F32)
@@ -224,7 +227,9 @@ def tile_list_msg_tanh_res_gate_kernel(
                 MULT,
             )
             if first + count == J:
-                nc.sync.dma_start(out[nt * P : (nt + 1) * P, :], windows[nt][:])
+                cuts = (0, T) if nt == 1 else (0, T // 4, T // 2, T)
+                for lo, hi in zip(cuts, cuts[1:]):
+                    nc.sync.dma_start(out[nt * P : (nt + 1) * P, lo:hi], windows[nt][:, lo:hi])
 
         picked = look_up_scales()
         move_scales(picked)

from contextlib import ExitStack

import concourse.mybir as mybir
from concourse.masks import make_identity

K, R, N, T, J = 1024, 512, 512, 2048, 1024
FLOPS = 2 * J * (2 * K * R + 2 * R * N)

F32 = mybir.dt.float32
BF16 = mybir.dt.bfloat16
I32 = mybir.dt.int32
U32 = mybir.dt.uint32
U16 = mybir.dt.uint16
U8 = mybir.dt.uint8
FP8X4 = mybir.dt.float8_e4m3fn_x4
FP4X4 = mybir.dt.float4_e2m1fn_x4
MULT = mybir.AluOpType.mult
TANH = mybir.ActivationFunctionType.Tanh
COPY = mybir.ActivationFunctionType.Copy

P = 128
PACK = 4
PASSES = K // (P * PACK)
QUADS = 4
CH = 512
CHUNKS = J // CH
LIST_COLS = J // 16
CH_COLS = CH // 16
N_TILES = N // P
GROUP = 256
PASS_ROWS = 16
SCALE_BASE = 96
SHORT = 3 * P


def tile_list_msg_tanh_res_gate_kernel(
    tc, tab_words, tab_scales, ws_words, ws_scales, wt_words, wt_scales, sm,
    wd4_words, wd4_scales, wd8_words, wd8_scales, gT, wgo, offs, offs2, out,
):
    nc = tc.nc
    with ExitStack() as ctx:
        keep = ctx.enter_context(tc.tile_pool(name="keep", bufs=1))
        psum = ctx.enter_context(tc.psum_pool(name="psum", bufs=1))

        def held(name, shape, dtype, tag=None):
            return keep.tile(shape, dtype, name=name, tag=tag or name, align_bytes=64)

        src_list = keep.tile([P, LIST_COLS], U16, name="src_list")
        dst_list = keep.tile([P, LIST_COLS], U16, name="dst_list")
        lists = (src_list, dst_list)

        tab_sc = held("tab_sc", [P, T // 4], I32)
        w1_sc = [held(f"w1_sc{w}", [P, PASSES, R // 4], I32) for w in range(2)]
        planes = held("planes", [P, PASSES, 2, J // 4], I32)
        wd_sc = held("wd_sc", [P, 2, N // 4], I32)
        windows = []

        def new_window(tag):
            window = held(f"window{len(windows)}", [P, T], F32, tag=tag)
            nc.gpsimd.memset(window[:], 0.0)
            windows.append(window)

        nc.vector.memset(w1_sc[0][:], 0)
        nc.vector.memset(tab_sc[0:SCALE_BASE, :], 0)
        nc.vector.memset(planes[:], 0)
        nc.vector.memset(w1_sc[1][:], 0)

        ident = held("ident", [P, P], F32)
        make_identity(nc, ident[:])

        nc.sync.dma_start(src_list[:], offs)
        nc.scalar.dma_start(tab_sc[SCALE_BASE:P, :], tab_scales.rearrange("a q t -> (a q) t").bitcast(I32))
        nc.sync.dma_start(dst_list[:], offs2)
        table = held("table", [P, T], I32)
        nc.sync.dma_start(table[:], tab_words[0].rearrange("p t b -> p (t b)").bitcast(I32))

        def load_w1_scales(w, r):
            scales = (ws_scales, wt_scales)[w]
            nc.sync.dma_start(
                w1_sc[w][r:P:32, :, :],
                scales.rearrange("a (q r) n -> r q a n", r=4)[r].bitcast(I32),
            )

        def load_w1_words(w):
            words = held(f"w1_words{w}", [P, PASSES, R // 2], I32)
            nc.sync.dma_start(words[:], (ws_words, wt_words)[w].rearrange("a p n -> p a n").bitcast(I32))
            return words

        def load_wd_scales(w, q):
            scales = (wd4_scales, wd8_scales)[w]
            nc.sync.dma_start(wd_sc[32 * q : 32 * q + 4, w, :], scales[0, 4 * q : 4 * q + 4, :].bitcast(I32))

        def load_gate_rows(nt):
            rows = held(f"g{nt}", [P, T], F32)
            nc.sync.dma_start(rows[:], gT[nt * P : (nt + 1) * P, :])
            return rows

        for r in range(4):
            load_w1_scales(0, r)
        for r in range(2):
            load_w1_scales(1, r)
        nc.gpsimd.memset(wd_sc[:], 0)
        new_window("window0")
        g_sb = {0: load_gate_rows(0)}
        for r in range(2, 4):
            load_w1_scales(1, r)
        wgo_dealt = held("wgo_dealt", [P, J // P], F32)
        nc.sync.dma_start(wgo_dealt[:], wgo[0].rearrange("(p c) -> p c", p=P))
        wgo_sb = held("wgo_sb", [P, J], F32)
        for u in range(2):
            spread = psum.tile([P, PACK, P], F32, name=f"spread{u}", tag=f"t{2 + u}")
            for c in range(PACK):
                column = wgo_dealt[:, PACK * u + c : PACK * u + c + 1]
                nc.tensor.transpose(spread[:, c, :], column.to_broadcast([P, P]), ident[:])
            nc.scalar.copy(
                wgo_sb[:].rearrange("m (p u c) -> m p u c", u=2, c=PACK)[:, :, u, :],
                spread[:].rearrange("m c p -> m p c"),
            )
        w1_words = [load_w1_words(w) for w in range(2)]

        def look_up_scales():
            picked = held("picked", [P, 2, J // 4], I32)
            for s in range(2):
                nc.vector.tensor_copy(picked[:, s, :].bitcast(U8), tab_sc[:].bitcast(U8).indirect(lists[s][:]))
            return picked

        def move_scales(picked):
            for a in range(PASSES):
                for r in range(4):
                    first = SCALE_BASE + PASS_ROWS * a + r
                    nc.sync.dma_start(planes[r:P:32, a, :, :], picked[first : first + 13 : 4, :, :])

        def look_up_words(c):
            both = []
            for s in range(2):
                tile = held(f"both{c}{s}", [P, CH], U32)
                nc.vector.tensor_copy(
                    tile[:], table[:].bitcast(U32).indirect(lists[s][:, c * CH_COLS : (c + 1) * CH_COLS])
                )
                both.append(tile)
            parted = []
            for s in range(2):
                apart = held(f"apart{c}{s}", [P, PASSES, CH], U16)
                nc.vector.tensor_copy(
                    apart[:], both[s][:].bitcast(U16).rearrange("p (j d) -> p d j", d=PASSES)
                )
                parted.append(apart)
            return parted

        def first_layer(jt, parted, tag):
            cols = slice((jt % 4) * P, (jt % 4 + 1) * P)
            acc = psum.tile([P, R], F32, name=f"acc{jt}", tag=tag)
            for i in range(2 * PASSES):
                s, a = divmod(i if jt == 0 else 2 * PASSES - 1 - i, PASSES)
                nc.tensor.matmul_mx(
                    out=acc[:],
                    lhsT=parted[s][:, a, cols].bitcast(FP4X4),
                    lhsT_scale=planes[:, a, s, :].bitcast(U8)[:, jt * P : (jt + 1) * P],
                    rhs=w1_words[s][:, a, :].bitcast(FP4X4),
                    rhs_scale=w1_sc[s][:, a, :].bitcast(U8),
                    start=(i == 0),
                    stop=(i == 2 * PASSES - 1),
                )
            th = held(f"th{jt}", [P, PACK, P], F32)
            nc.scalar.activation(th[:], acc[:].rearrange("j (m t) -> j t m", t=PACK), TANH)
            return th

        def hidden(name, ths, h_grouped, tags, h_rows):
            per_bank = PACK // len(ths)
            banks = [psum.tile([P, per_bank, len(ths) * P], F32, name=f"turned{name}{tag}", tag=tag) for tag in tags]
            for t in range(PACK):
                for i, th in enumerate(ths):
                    nc.tensor.transpose(
                        banks[t // per_bank][:, t % per_bank, i * P : (i + 1) * P], th[:, t, :], ident[:]
                    )
            for t in range(PACK):
                nc.scalar.activation(
                    h_rows[:, t, :], banks[t // per_bank][:, t % per_bank, :], COPY, scale=sm_sb[:, t : t + 1]
                )
            nc.scalar.copy(
                h_grouped.rearrange("p (c i) t -> p c t i", i=4), h_rows.rearrange("p t (c i) -> p c t i", i=4)
            )

        def quantise(c, cols):
            nc.vector.quantize_mx(
                out=codes[c][:, cols].bitcast(FP8X4),
                scales=h_sc[c][:, cols],
                in_=grouped[c][:, cols, :].rearrange("p j t -> p (j t)"),
            )

        def gate(nt, tag=None):
            tile = held(f"gate{nt}", [P, J], F32, tag=tag)
            nc.vector.tensor_tensor(tile[:], g_sb[nt][:].indirect(src_list[:]), wgo_sb[:], MULT)
            return tile

        def second_layer(nt, c, cols, y):
            rows = slice(nt * P, (nt + 1) * P)
            weights = (wd4[:, nt * P // 2 : (nt + 1) * P // 2].bitcast(FP4X4), wd8[:, rows].bitcast(FP8X4))
            for w in range(2):
                nc.tensor.matmul_mx(
                    out=y,
                    lhsT=weights[w],
                    lhsT_scale=wd_sc[:, w, :].bitcast(U8)[:, rows],
                    rhs=codes[c][:, cols].bitcast(FP8X4),
                    rhs_scale=h_sc[c][:, cols],
                    start=(w == 0),
                    stop=(w == 1),
                )

        def message(nt, c, tag, y_sb):
            y = psum.tile([P, CH], F32, name=f"y{nt}{c}", tag=tag)
            second_layer(nt, c, slice(0, CH), y[:])
            nc.scalar.copy(y_sb, y[:])

        def short_message(nt, tag, cols):
            y = psum.tile([P, cols.stop - cols.start], F32, name=f"y_short{nt}{tag}", tag=tag)
            for first in range(cols.start, cols.stop, P):
                second_layer(nt, 0, slice(first, first + P), y[:, first - cols.start : first - cols.start + P])
            nc.scalar.copy(early[nt][:, cols], y[:])

        def scatter(nt, first, y_sb):
            count = y_sb.shape[1]
            nc.vector.tensor_tensor(
                windows[nt][:].indirect(dst_list[:, first // 16 : (first + count) // 16]),
                y_sb,
                gates[nt][:, first : first + count],
                MULT,
            )
            if first + count == J:
                cuts = (0, T) if nt == 1 else (0, T // 4, T // 2, T)
                for lo, hi in zip(cuts, cuts[1:]):
                    nc.sync.dma_start(out[nt * P : (nt + 1) * P, lo:hi], windows[nt][:, lo:hi])

        picked = look_up_scales()
        move_scales(picked)
        parted_0 = look_up_words(0)
        parted_1 = look_up_words(1)

        sm_sb = held("sm_sb", [P, PACK], F32)
        nc.sync.dma_start(sm_sb[:], sm.rearrange("(p t) -> p t", t=PACK))
        for nt in range(1, N_TILES):
            g_sb[nt] = load_gate_rows(nt)
        for q in range(QUADS):
            load_wd_scales(0, q)
        wd8 = held("wd8", [P, N], I32)
        nc.sync.dma_start(wd8[:], wd8_words[0].rearrange("p n i -> p (n i)").bitcast(I32))
        wd4 = held("wd4", [P, N // 2], I32)
        nc.sync.dma_start(wd4[:], wd4_words[0].bitcast(I32))
        for q in range(QUADS):
            load_wd_scales(1, q)

        grouped = [held(f"h_grouped{c}", [P, CH, PACK], BF16) for c in range(CHUNKS)]
        codes = [held(f"h_codes{c}", [P, CH], U32) for c in range(CHUNKS)]
        h_sc = [held(f"h_sc{c}", [P, CH], U8) for c in range(CHUNKS)]
        ths = [first_layer(0, parted_0, "a0")]
        for jt in range(4):
            if jt < 2:
                ths.append(first_layer(jt + 1, parted_0, f"a{jt + 1}"))
            if jt == 3:
                ths.append(first_layer(jt, parted_0, f"a{jt}"))
            rows = held(f"h_early{jt}", [P, PACK, P], BF16)
            hidden(f"early{jt}", [ths[jt]], grouped[0][:, jt * P : (jt + 1) * P, :], (f"t{jt}",), rows[:])
        ths_late = [first_layer(jt, parted_1, f"a{jt - 4}") for jt in range(4, 7)]
        new_window("both11")
        gates = [gate(0)]
        new_window("g0")
        gates.extend([gate(1), gate(2)])
        quantise(0, slice(0, SHORT))
        gates.append(gate(3, tag="h_early2"))
        quantise(0, slice(SHORT, CH))
        new_window("h_grouped0")
        early = [held(f"y_early{nt}", [P, SHORT], F32) for nt in range(2)]
        short_message(0, "t0", slice(0, GROUP))
        short_message(0, "t2", slice(GROUP, SHORT))
        short_message(1, "t1", slice(0, SHORT))
        rows = held("h_rows2", [P, PACK, GROUP], BF16)
        hidden(2, ths_late[0:2], grouped[1][:, 0:GROUP, :], ("t0", "t2"), rows[:])
        ths_late.append(first_layer(7, parted_1, "t1"))
        y_2 = held("y_2", [P, CH], F32)
        message(2, 0, "t0", y_2[:])
        rows = held("h_rows3", [P, PACK, GROUP], BF16)
        hidden(3, ths_late[2:4], grouped[1][:, GROUP:CH, :], ("t2", "t1"), rows[:])
        for nt in range(2):
            scatter(nt, 0, early[nt][:])
        scatter(2, 0, y_2[:])
        quantise(1, slice(0, CH))
        rest = J - SHORT
        late = held("y_late", [P, CH + 2 * rest], F32, tag="h_rows3")
        message(3, 0, "t2", late[:, 0:CH])
        scatter(3, 0, late[:, 0:CH])
        long_rows = late[:, CH:].rearrange("p (n j) -> p n j", n=2)
        fourth = psum.tile([P, 2, P], F32, name="y_fourth", tag="t1")
        for nt in range(2):
            second_layer(nt, 0, slice(SHORT, CH), fourth[:, nt, :])
        nc.scalar.copy(long_rows[:, :, 0:P], fourth[:])
        for nt in range(2, N_TILES):
            y_sb = held(f"y_end{nt}", [P, CH], F32)
            message(nt, 1, f"a{nt}", y_sb[:])
            scatter(nt, CH, y_sb[:])
        for nt in range(2):
            message(nt, 1, f"a{nt}", long_rows[:, nt, P:])
            scatter(nt, SHORT, long_rows[:, nt, :])
